import numpy as np
import ml_dtypes


def mxq(x, axis, fmt="e4m3"):
    dtype, down = {"e4m3": (ml_dtypes.float8_e4m3fn, 7), "e5m2": (ml_dtypes.float8_e5m2, 14)}[fmt]
    v = np.moveaxis(np.asarray(x, np.float32).astype(ml_dtypes.bfloat16).astype(np.float64), axis, -1)
    blocks = v.reshape(v.shape[:-1] + (-1, 32))
    amax = np.abs(blocks).max(-1, keepdims=True)
    byte = np.maximum(np.where(amax > 0, np.frexp(amax)[1] - 1 + 127, 0) - down, 1)
    scale = np.exp2(byte - 127.0)
    codes = (blocks / scale).astype(np.float32).astype(dtype).astype(np.float64)
    return np.moveaxis((codes * scale).reshape(v.shape), -1, axis)


WIDE = False


def mx_kscale(k, group=512):
    if not WIDE:
        return np.ones(k)
    levels = np.array([10, -10, 5, -5, 0])
    if group != 512:
        return np.exp2(np.random.permutation(np.resize(levels, k // group))).repeat(group)
    if k % 512:
        return np.exp2(np.random.permutation(np.resize(levels, k // 32))).repeat(32)
    a = np.empty((k // 512, 16))
    for p in range(k // 512):
        a[p, :8] = np.random.permutation(np.resize(levels, 8))
        for g in range(8):
            far = levels[np.abs(levels - a[p, g]) >= 10]
            a[p, g + 8] = far[np.random.randint(len(far))]
    return np.exp2(a.ravel()).repeat(32)


def f64(x):
    return np.asarray(x).astype(np.float64)


def striped(idx):
    return np.tile(np.asarray(idx).reshape(-1, 16).T, (8, 1)).astype(np.uint16)


def unstriped(offs):
    return offs[:16].T.reshape(-1).astype(np.int64)


H, KV, D, NQ, N = 8, 8, 128, 512, 512


def setup_inputs():
    n = np.random.standard_normal
    s = mx_kscale(D, 0)[:, None]
    u = mx_kscale(N)
    t = np.random.uniform(0.5, 2.0, N) * u
    v = n((KV, N, 128))
    return {
        "qT": (n((H, D, NQ)) * s * (0.70 / np.sqrt(D))).astype(np.float32),
        "kT": (n((KV, D, N)) / s).astype(np.float32),
        "t": t.reshape(N, 1).astype(np.float32),
        "v": (v / t[:, None]).astype(np.float32),
        "kb": (0.5 * n((N, 1))).astype(np.float32),
        "gn": np.tile(np.random.uniform(0.5, 2.0, 128), (128, 1)).astype(np.float32),
    }


def reference(qT, kT, t, v, kb, gn):
    a = mxq(f64(kT), 1, "e4m3").transpose(0, 2, 1) @ mxq(f64(qT), 1, "e4m3")
    a = a + f64(kb)
    p = a / (1.0 + np.exp(-a))
    w = p * f64(t)
    y = mxq(w, 1, "e4m3").transpose(0, 2, 1) @ mxq(f64(v), 1, "e4m3")
    y = y / 16.0
    y = y / np.sqrt(np.mean(np.square(y), -1, keepdims=True) + 1e-5) * f64(gn)[:1]
    return y

@@ -1,0 +1,296 @@
+from contextlib import ExitStack
+
+import concourse.mybir as mybir
+
+H, D, NQ, N = 8, 128, 512, 512
+FLOPS = 2 * 2 * H * NQ * N * D
+
+F32 = mybir.dt.float32
+BF16 = mybir.dt.bfloat16
+U32 = mybir.dt.uint32
+U8 = mybir.dt.uint8
+FP8X4 = mybir.dt.float8_e4m3fn_x4
+ACT = mybir.ActivationFunctionType
+ALU = mybir.AluOpType
+
+P = 128
+PACK = 4
+SIDE = 4
+ROWS = P // SIDE
+HALF = NQ // 2
+EPS = 1e-5 * 16.0 * 16.0
+
+
+def tile_rows_a_silu_kb_onorm_kernel(tc, qT, kT, t, v, kb, gn, out):
+    nc = tc.nc
+    with ExitStack() as ctx:
+        sb = ctx.enter_context(tc.tile_pool(name="sb", bufs=1))
+        ps = ctx.enter_context(tc.psum_pool(name="ps", bufs=1))
+        ctx.enter_context(tc.manual_schedule())
+
+        def mx_tiles(name):
+            codes = sb.tile([P, 2 * P], U32, name=name + "_codes", align_bytes=64)
+            scales = sb.tile([P, 2 * P], U8, name=name + "_scales", align_bytes=64)
+            return codes, scales
+
+        def quantize(mx, grouped):
+            nc.vector.quantize_mx(out=mx[0][:].bitcast(FP8X4), scales=mx[1][:], in_=grouped[:])
+
+        q_raw, k_raw, v_raw = {}, {}, {}
+
+        def load_q(s, u):
+            q_raw[s, u] = sb.tile([P, PACK, HALF], F32, name="q_raw%d%d" % (s, u))
+            src = qT[SIDE * s : SIDE * (s + 1)].rearrange("h (p j) n -> (h p) j n", j=PACK)
+            nc.sync.dma_start(out=q_raw[s, u][:], in_=src[:, :, HALF * u : HALF * (u + 1)])
+
+        def load_k(s):
+            k_raw[s] = sb.tile([P, PACK, N], F32, name="k_raw%d" % s)
+            src = kT[SIDE * s : SIDE * (s + 1)].rearrange("h (p j) n -> (h p) j n", j=PACK)
+            nc.sync.dma_start(out=k_raw[s][:], in_=src)
+
+        def load_v(s):
+            v_raw[s] = sb.tile([P, SIDE, PACK * D], F32, name="v_raw%d" % s)
+            src = v[SIDE * s : SIDE * (s + 1)].rearrange("h (p j) e -> p h (j e)", j=PACK)
+            nc.sync.dma_start(out=v_raw[s][:], in_=src)
+
+        kb_sb = sb.tile([P, PACK], F32)
+        t_sb = sb.tile([P, PACK], F32)
+        gn_sb = sb.tile([P, D], F32)
+
+        load_q(0, 0)
+        load_k(0)
+        nc.sync.dma_start(out=kb_sb[:], in_=kb.rearrange("(p j) o -> p (j o)", j=PACK))
+        load_q(0, 1)
+        nc.sync.dma_start(out=t_sb[:], in_=t.rearrange("(p j) o -> p (j o)", j=PACK))
+        load_k(1)
+        load_q(1, 0)
+        load_q(1, 1)
+        load_v(0)
+        load_v(1)
+        nc.sync.dma_start(out=gn_sb[:], in_=gn)
+
+        grouped, q_mx, k_mx, v_mx, w_mx = {}, {}, {}, {}, {}
+
+        def group_q(s, u):
+            g = sb.tile([P, HALF * PACK], BF16, name="q_grp%d%d" % (s, u), align_bytes=64)
+            grouped["q", s, u] = g
+            nc.vector.tensor_copy(
+                out=g[:].rearrange("p (c m n j) -> p m j n c", c=2, n=2, j=PACK),
+                in_=q_raw[s, u][:].rearrange("p j (m n c) -> p m j n c", n=2, c=2),
+            )
+
+        def quant_q(s, u):
+            q_mx[s, u] = mx_tiles("q%d%d" % (s, u))
+            quantize(q_mx[s, u], grouped["q", s, u])
+
+        def group_k(s, a):
+            g = sb.tile([P, 2 * P * PACK], BF16, name="k_grp%d%d" % (s, a), align_bytes=64)
+            grouped["k", s, a] = g
+            nc.vector.tensor_copy(
+                out=g[:].rearrange("p (r m j) -> p m j r", r=2, j=PACK),
+                in_=k_raw[s][:].rearrange("p j (m r) -> p m j r", r=PACK)[:, :, :, 2 * a : 2 * a + 2],
+            )
+
+        def quant_k(s, a):
+            k_mx[s, a] = mx_tiles("k%d%d" % (s, a))
+            quantize(k_mx[s, a], grouped["k", s, a])
+
+        def group_v(pair, copy):
+            g = sb.tile([P, 2 * D * PACK], BF16, name="v_grp%d" % pair, align_bytes=64)
+            grouped["v", pair] = g
+            first = 2 * (pair % 2)
+            copy(
+                out=g[:].rearrange("p (h c i j) -> p h c j i", h=2, i=4, j=PACK),
+                in_=v_raw[pair // 2][:, first : first + 2, :].rearrange("p h (j c i) -> p h c j i", j=PACK, i=4),
+            )
+
+        def quant_v(pair):
+            v_mx[pair] = mx_tiles("v%d" % pair)
+            quantize(v_mx[pair], grouped["v", pair])
+
+        score_banks = []
+        y_banks = []
+        for g in range(SIDE):
+            score_banks.append(ps.tile([P, 2, HALF], F32, name="scores%d" % g))
+            y_banks.append(ps.tile([P, PACK, D], F32, name="y%d" % g))
+
+        def fill_of(i):
+            return i // 16, (i // 8) % 2, (i // 4) % 2, i % 4
+
+        def score_call(i, call):
+            s, u, a, g = fill_of(i)
+            r, c = divmod(call, 2)
+            rows = slice(ROWS * g, ROWS * (g + 1))
+            kc = slice(P * r, P * (r + 1))
+            qc = slice(P * c, P * (c + 1))
+            nc.tensor.matmul_mx(
+                out=score_banks[g][:, r, qc],
+                lhsT=k_mx[s, a][0][rows, kc].bitcast(FP8X4),
+                lhsT_scale=k_mx[s, a][1][rows, kc],
+                rhs=q_mx[s, u][0][rows, qc].bitcast(FP8X4),
+                rhs_scale=q_mx[s, u][1][rows, qc],
+                start=True,
+                stop=True,
+            )
+
+        p_sb = {}
+
+        def silu(i):
+            s, u, a, g = fill_of(i)
+            n = 8 * s + 4 * u + g
+            if a == 0:
+                p_sb[n] = sb.tile([P, PACK, HALF], F32, name="p%d" % n)
+            for r in range(2):
+                place = 2 * a + r
+                nc.scalar.activation(
+                    out=p_sb[n][:, place, :],
+                    in_=score_banks[g][:, r, :],
+                    func=ACT.Silu,
+                    bias=kb_sb[:, place : place + 1],
+                )
+
+        def fills(first, last):
+            for i in range(first, last):
+                for call in range(2):
+                    score_call(i, 2 + call)
+                    if i + 1 < 32:
+                        score_call(i + 1, call)
+                silu(i)
+
+        def weigh(n):
+            w = sb.tile([P, HALF * PACK], BF16, name="w_grp", tag="w_grp", bufs=3, align_bytes=64)
+            grouped["w", n] = w
+            nc.vector.tensor_tensor(
+                out=w[:].rearrange("p (c i r) -> p c r i", i=4, r=PACK),
+                in0=p_sb[n][:].rearrange("p r (c i) -> p c r i", i=4),
+                in1=t_sb[:].unsqueeze(1).unsqueeze(3).to_broadcast([P, HALF // 4, PACK, 4]),
+                op=ALU.mult,
+            )
+
+        def quant_w(n):
+            w_mx[n] = mx_tiles("w%d" % n)
+            quantize(w_mx[n], grouped["w", n])
+
+        def values(h, u):
+            s, g = divmod(h, SIDE)
+            n = 8 * s + 4 * u + g
+            vc = slice(D * (h % 2), D * (h % 2 + 1))
+            for c in range(2):
+                qc = slice(P * c, P * (c + 1))
+                nc.tensor.matmul_mx(
+                    out=y_banks[g][:, 2 * u + c, :],
+                    lhsT=w_mx[n][0][:, qc].bitcast(FP8X4),
+                    lhsT_scale=w_mx[n][1][:, qc],
+                    rhs=v_mx[h // 2][0][:, vc].bitcast(FP8X4),
+                    rhs_scale=v_mx[h // 2][1][:, vc],
+                    start=True,
+                    stop=True,
+                )
+
+        rstd = {}
+
+        def norm(h):
+            ssq = sb.tile([P, PACK], F32, name="ssq%d" % h)
+            squares = sb.tile([P, PACK, D], F32, name="squares", tag="squares", bufs=2)
+            for j in range(PACK):
+                nc.scalar.activation(
+                    out=squares[:, j, :],
+                    in_=y_banks[h % SIDE][:, j, :],
+                    func=ACT.Square,
+                    accum_out=ssq[:, j : j + 1],
+                )
+            rstd[h] = sb.tile([P, PACK], F32, name="rstd%d" % h)
+            nc.scalar.activation(
+                out=rstd[h][:], in_=ssq[:], func=ACT.Abs_reciprocal_sqrt, scale=1.0 / D, bias=EPS
+            )
+
+        def finish(h):
+            o = sb.tile([P, 2, 2 * D], F32, name="o%d" % h)
+            for j in range(PACK):
+                u, c = divmod(j, 2)
+                nc.vector.scalar_tensor_tensor(
+                    out=o[:, u, D * c : D * (c + 1)],
+                    in0=y_banks[h % SIDE][:, j, :],
+                    scalar=rstd[h][:, j : j + 1],
+                    in1=gn_sb[:],
+                    op0=ALU.mult,
+                    op1=ALU.mult,
+                )
+            nc.sync.dma_start(out=out[h].rearrange("(u m c) e -> m u (c e)", u=2, c=2), in_=o[:])
+
+        group_q(0, 0)
+        quant_q(0, 0)
+        group_k(0, 0)
+        quant_k(0, 0)
+        group_k(0, 1)
+        group_q(0, 1)
+        quant_k(0, 1)
+        quant_q(0, 1)
+        group_k(1, 0)
+        group_k(1, 1)
+        quant_k(1, 0)
+
+        score_call(0, 0)
+        score_call(0, 1)
+        fills(0, 8)
+
+        weigh(0)
+        quant_k(1, 1)
+        group_q(1, 0)
+        weigh(1)
+        quant_q(1, 0)
+        quant_w(0)
+        group_q(1, 1)
+        weigh(2)
+        quant_w(1)
+        quant_q(1, 1)
+        weigh(3)
+        quant_w(2)
+
+        fills(8, 16)
+        group_v(0, nc.scalar.copy)
+        group_v(1, nc.scalar.copy)
+        for n in range(4, 8):
+            weigh(n)
+            quant_w(n - 1)
+        quant_v(0)
+        quant_v(1)
+
+        fills(16, 24)
+        for n in range(8, 12):
+            weigh(n)
+            quant_w(n - 1)
+
+        fills(24, 32)
+        for h in range(SIDE):
+            values(h, 0)
+            values(h, 1)
+
+        norm(0)
+        norm(1)
+        group_v(2, nc.scalar.copy)
+        norm(2)
+        norm(3)
+
+        weigh(12)
+        quant_w(11)
+        weigh(13)
+        quant_w(12)
+        group_v(3, nc.vector.tensor_copy)
+        finish(0)
+        weigh(14)
+        quant_w(13)
+        finish(1)
+        quant_v(2)
+        weigh(15)
+        quant_v(3)
+        quant_w(14)
+        finish(2)
+        quant_w(15)
+        finish(3)
+
+        for h in range(SIDE, H):
+            values(h, 0)
+            values(h, 1)
+            norm(h)
+            finish(h)

@@ -17,7 +17,7 @@ P = 128
 PACK = 4
 SIDE = 4
 ROWS = P // SIDE
-HALF = NQ // 2
+TILES = NQ // P
 EPS = 1e-5 * 16.0 * 16.0
 
 
@@ -28,269 +28,297 @@ def tile_rows_a_silu_kb_onorm_kernel(tc, qT, kT, t, v, kb, gn, out):
         ps = ctx.enter_context(tc.psum_pool(name="ps", bufs=1))
         ctx.enter_context(tc.manual_schedule())
 
-        def mx_tiles(name):
-            codes = sb.tile([P, 2 * P], U32, name=name + "_codes", align_bytes=64)
-            scales = sb.tile([P, 2 * P], U8, name=name + "_scales", align_bytes=64)
+        def quantize(name, grouped, words):
+            codes = sb.tile([P, words], U32, name=name + "_codes", align_bytes=64)
+            scales = sb.tile([P, words], U8, name=name + "_scales", align_bytes=64)
+            nc.vector.quantize_mx(out=codes[:].bitcast(FP8X4), scales=scales[:], in_=grouped)
             return codes, scales
 
-        def quantize(mx, grouped):
-            nc.vector.quantize_mx(out=mx[0][:].bitcast(FP8X4), scales=mx[1][:], in_=grouped[:])
-
-        q_raw, k_raw, v_raw = {}, {}, {}
-
-        def load_q(s, u):
-            q_raw[s, u] = sb.tile([P, PACK, HALF], F32, name="q_raw%d%d" % (s, u))
-            src = qT[SIDE * s : SIDE * (s + 1)].rearrange("h (p j) n -> (h p) j n", j=PACK)
-            nc.sync.dma_start(out=q_raw[s, u][:], in_=src[:, :, HALF * u : HALF * (u + 1)])
-
-        def load_k(s):
-            k_raw[s] = sb.tile([P, PACK, N], F32, name="k_raw%d" % s)
-            src = kT[SIDE * s : SIDE * (s + 1)].rearrange("h (p j) n -> (h p) j n", j=PACK)
-            nc.sync.dma_start(out=k_raw[s][:], in_=src)
+        def load_features(name, x, s, first, last):
+            raw = sb.tile([P, PACK, last - first], F32, name=name)
+            src = x[SIDE * s : SIDE * (s + 1)].rearrange("h (p j) n -> (h p) j n", j=PACK)
+            nc.sync.dma_start(out=raw[:], in_=src[:, :, first:last])
+            return raw
 
         def load_v(s):
-            v_raw[s] = sb.tile([P, SIDE, PACK * D], F32, name="v_raw%d" % s)
+            raw = sb.tile([P, SIDE, PACK * D], F32, name="v_raw%d" % s)
             src = v[SIDE * s : SIDE * (s + 1)].rearrange("h (p j) e -> p h (j e)", j=PACK)
-            nc.sync.dma_start(out=v_raw[s][:], in_=src)
+            nc.sync.dma_start(out=raw[:], in_=src)
+            return raw
 
         kb_sb = sb.tile([P, PACK], F32)
         t_sb = sb.tile([P, PACK], F32)
         gn_sb = sb.tile([P, D], F32)
 
-        load_q(0, 0)
-        load_k(0)
+        k0_low = load_features("k0_low", kT, 0, 0, N // 2)
+        k0_high = load_features("k0_high", kT, 0, N // 2, N)
+        q0_first = load_features("q0_first", qT, 0, 0, P)
         nc.sync.dma_start(out=kb_sb[:], in_=kb.rearrange("(p j) o -> p (j o)", j=PACK))
-        load_q(0, 1)
         nc.sync.dma_start(out=t_sb[:], in_=t.rearrange("(p j) o -> p (j o)", j=PACK))
-        load_k(1)
-        load_q(1, 0)
-        load_q(1, 1)
-        load_v(0)
-        load_v(1)
+        q0_rest = load_features("q0_rest", qT, 0, P, NQ)
+        k1_raw = load_features("k1_raw", kT, 1, 0, N)
+        q1_raw = load_features("q1_raw", qT, 1, 0, NQ)
+        v_raw = [load_v(0), load_v(1)]
         nc.sync.dma_start(out=gn_sb[:], in_=gn)
 
         grouped, q_mx, k_mx, v_mx, w_mx = {}, {}, {}, {}, {}
 
-        def group_q(s, u):
-            g = sb.tile([P, HALF * PACK], BF16, name="q_grp%d%d" % (s, u), align_bytes=64)
-            grouped["q", s, u] = g
+        def group_q(s, j0, tiles, raw):
+            g = sb.tile([P, tiles * P * PACK], BF16, name="q_grp%d%d" % (s, j0), align_bytes=64)
+            grouped["q", s, j0] = g
             nc.vector.tensor_copy(
-                out=g[:].rearrange("p (c m n j) -> p m j n c", c=2, n=2, j=PACK),
-                in_=q_raw[s, u][:].rearrange("p j (m n c) -> p m j n c", n=2, c=2),
+                out=g[:].rearrange("p (c i j) -> p c j i", i=2, j=PACK),
+                in_=raw.rearrange("p j (c i) -> p c j i", i=2),
             )
 
-        def quant_q(s, u):
-            q_mx[s, u] = mx_tiles("q%d%d" % (s, u))
-            quantize(q_mx[s, u], grouped["q", s, u])
+        def quant_q(s, j0, tiles):
+            mx = quantize("q%d%d" % (s, j0), grouped["q", s, j0][:], tiles * P)
+            for c in range(tiles):
+                q_mx[s, j0 + c] = (mx, slice(P * c, P * (c + 1)))
 
-        def group_k(s, a):
-            g = sb.tile([P, 2 * P * PACK], BF16, name="k_grp%d%d" % (s, a), align_bytes=64)
-            grouped["k", s, a] = g
+        def group_k(s, a, raw, m0):
+            if m0 == 0:
+                grouped["k", s, a] = sb.tile([P, 2 * P * PACK], BF16, name="k_grp%d%d" % (s, a), align_bytes=64)
+            count = raw.shape[2] // PACK
             nc.vector.tensor_copy(
-                out=g[:].rearrange("p (r m j) -> p m j r", r=2, j=PACK),
-                in_=k_raw[s][:].rearrange("p j (m r) -> p m j r", r=PACK)[:, :, :, 2 * a : 2 * a + 2],
+                out=grouped["k", s, a][:].rearrange("p (r m j) -> p m j r", r=2, j=PACK)[:, m0 : m0 + count],
+                in_=raw[:].rearrange("p j (m r) -> p m j r", r=PACK)[:, :, :, 2 * a : 2 * a + 2],
             )
 
         def quant_k(s, a):
-            k_mx[s, a] = mx_tiles("k%d%d" % (s, a))
-            quantize(k_mx[s, a], grouped["k", s, a])
+            mx = quantize("k%d%d" % (s, a), grouped["k", s, a][:], 2 * P)
+            for r in range(2):
+                k_mx[s, 2 * a + r] = (mx, slice(P * r, P * (r + 1)))
 
-        def group_v(pair, copy):
-            g = sb.tile([P, 2 * D * PACK], BF16, name="v_grp%d" % pair, align_bytes=64)
-            grouped["v", pair] = g
-            first = 2 * (pair % 2)
+        def group_v(h, copy):
+            if h % 2 == 0:
+                grouped["v", h // 2] = sb.tile([P, 2, D * PACK], BF16, name="v_grp%d" % (h // 2), align_bytes=64)
             copy(
-                out=g[:].rearrange("p (h c i j) -> p h c j i", h=2, i=4, j=PACK),
-                in_=v_raw[pair // 2][:, first : first + 2, :].rearrange("p h (j c i) -> p h c j i", j=PACK, i=4),
+                out=grouped["v", h // 2][:, h % 2, :].rearrange("p (c i j) -> p c j i", i=2, j=PACK),
+                in_=v_raw[h // SIDE][:, h % SIDE, :].rearrange("p (j c i) -> p c j i", j=PACK, i=2),
             )
 
         def quant_v(pair):
-            v_mx[pair] = mx_tiles("v%d" % pair)
-            quantize(v_mx[pair], grouped["v", pair])
+            v_mx[pair] = quantize("v%d" % pair, grouped["v", pair][:].rearrange("p h x -> p (h x)"), 2 * D)
 
         score_banks = []
         y_banks = []
         for g in range(SIDE):
-            score_banks.append(ps.tile([P, 2, HALF], F32, name="scores%d" % g))
-            y_banks.append(ps.tile([P, PACK, D], F32, name="y%d" % g))
-
-        def fill_of(i):
-            return i // 16, (i // 8) % 2, (i // 4) % 2, i % 4
-
-        def score_call(i, call):
-            s, u, a, g = fill_of(i)
-            r, c = divmod(call, 2)
-            rows = slice(ROWS * g, ROWS * (g + 1))
-            kc = slice(P * r, P * (r + 1))
-            qc = slice(P * c, P * (c + 1))
-            nc.tensor.matmul_mx(
-                out=score_banks[g][:, r, qc],
-                lhsT=k_mx[s, a][0][rows, kc].bitcast(FP8X4),
-                lhsT_scale=k_mx[s, a][1][rows, kc],
-                rhs=q_mx[s, u][0][rows, qc].bitcast(FP8X4),
-                rhs_scale=q_mx[s, u][1][rows, qc],
-                start=True,
-                stop=True,
-            )
+            score_banks.append(ps.tile([P, PACK * P], F32, name="scores%d" % g))
+            y_banks.append(ps.tile([P, TILES, D], F32, name="y%d" % g))
 
         p_sb = {}
 
-        def silu(i):
-            s, u, a, g = fill_of(i)
-            n = 8 * s + 4 * u + g
-            if a == 0:
-                p_sb[n] = sb.tile([P, PACK, HALF], F32, name="p%d" % n)
-            for r in range(2):
-                place = 2 * a + r
+        def fill(h, places, j0, tiles):
+            s, g = divmod(h, SIDE)
+            rows = slice(ROWS * g, ROWS * (g + 1))
+            width = tiles * P
+            for x, r in enumerate(places):
+                k_tiles, kc = k_mx[s, r]
+                for c in range(tiles):
+                    q_tiles, qc = q_mx[s, j0 + c]
+                    nc.tensor.matmul_mx(
+                        out=score_banks[g][:, width * x + P * c : width * x + P * (c + 1)],
+                        lhsT=k_tiles[0][rows, kc].bitcast(FP8X4),
+                        lhsT_scale=k_tiles[1][rows, kc],
+                        rhs=q_tiles[0][rows, qc].bitcast(FP8X4),
+                        rhs_scale=q_tiles[1][rows, qc],
+                        start=True,
+                        stop=True,
+                    )
+            if places[0] == 0:
+                p_sb[h, j0] = sb.tile([P, PACK, width], F32, name="p%d%d" % (h, j0))
+            for x, r in enumerate(places):
                 nc.scalar.activation(
-                    out=p_sb[n][:, place, :],
-                    in_=score_banks[g][:, r, :],
+                    out=p_sb[h, j0][:, r, :],
+                    in_=score_banks[g][:, width * x : width * (x + 1)],
                     func=ACT.Silu,
-                    bias=kb_sb[:, place : place + 1],
+                    bias=kb_sb[:, r : r + 1],
                 )
 
-        def fills(first, last):
-            for i in range(first, last):
-                for call in range(2):
-                    score_call(i, 2 + call)
-                    if i + 1 < 32:
-                        score_call(i + 1, call)
-                silu(i)
-
-        def weigh(n):
-            w = sb.tile([P, HALF * PACK], BF16, name="w_grp", tag="w_grp", bufs=3, align_bytes=64)
-            grouped["w", n] = w
+        def weigh(h, j0, tiles, p_part):
+            w = sb.tile([P, tiles * P * PACK], BF16, name="w_grp", tag="w_grp", bufs=3, align_bytes=64)
+            grouped["w", h, j0] = w
             nc.vector.tensor_tensor(
-                out=w[:].rearrange("p (c i r) -> p c r i", i=4, r=PACK),
-                in0=p_sb[n][:].rearrange("p r (c i) -> p c r i", i=4),
-                in1=t_sb[:].unsqueeze(1).unsqueeze(3).to_broadcast([P, HALF // 4, PACK, 4]),
+                out=w[:].rearrange("p (c i r) -> p c r i", i=2, r=PACK),
+                in0=p_part.rearrange("p r (c i) -> p c r i", i=2),
+                in1=t_sb[:].unsqueeze(1).unsqueeze(3).to_broadcast([P, tiles * P // 2, PACK, 2]),
                 op=ALU.mult,
             )
 
-        def quant_w(n):
-            w_mx[n] = mx_tiles("w%d" % n)
-            quantize(w_mx[n], grouped["w", n])
+        def quant_w(h, j0, tiles):
+            mx = quantize("w%d%d" % (h, j0), grouped["w", h, j0][:], tiles * P)
+            for c in range(tiles):
+                w_mx[h, j0 + c] = (mx, slice(P * c, P * (c + 1)))
 
-        def values(h, u):
-            s, g = divmod(h, SIDE)
-            n = 8 * s + 4 * u + g
+        def values(h, first, last):
             vc = slice(D * (h % 2), D * (h % 2 + 1))
-            for c in range(2):
-                qc = slice(P * c, P * (c + 1))
+            for j in range(first, last):
+                w_tiles, wc = w_mx[h, j]
                 nc.tensor.matmul_mx(
-                    out=y_banks[g][:, 2 * u + c, :],
-                    lhsT=w_mx[n][0][:, qc].bitcast(FP8X4),
-                    lhsT_scale=w_mx[n][1][:, qc],
+                    out=y_banks[h % SIDE][:, j, :],
+                    lhsT=w_tiles[0][:, wc].bitcast(FP8X4),
+                    lhsT_scale=w_tiles[1][:, wc],
                     rhs=v_mx[h // 2][0][:, vc].bitcast(FP8X4),
                     rhs_scale=v_mx[h // 2][1][:, vc],
                     start=True,
                     stop=True,
                 )
 
-        rstd = {}
+        ssq, rstd = {}, {}
 
-        def norm(h):
-            ssq = sb.tile([P, PACK], F32, name="ssq%d" % h)
-            squares = sb.tile([P, PACK, D], F32, name="squares", tag="squares", bufs=2)
-            for j in range(PACK):
+        def squares(h, first, last):
+            if first == 0:
+                ssq[h] = sb.tile([P, TILES], F32, name="ssq%d" % h)
+            for j in range(first, last):
+                sq = sb.tile([P, D], F32, name="sq", tag="sq", bufs=4)
                 nc.scalar.activation(
-                    out=squares[:, j, :],
+                    out=sq[:],
                     in_=y_banks[h % SIDE][:, j, :],
                     func=ACT.Square,
-                    accum_out=ssq[:, j : j + 1],
+                    accum_out=ssq[h][:, j : j + 1],
                 )
-            rstd[h] = sb.tile([P, PACK], F32, name="rstd%d" % h)
+
+        def root(h):
+            rstd[h] = sb.tile([P, TILES], F32, name="rstd%d" % h)
             nc.scalar.activation(
-                out=rstd[h][:], in_=ssq[:], func=ACT.Abs_reciprocal_sqrt, scale=1.0 / D, bias=EPS
+                out=rstd[h][:], in_=ssq[h][:], func=ACT.Abs_reciprocal_sqrt, scale=1.0 / D, bias=EPS
             )
 
-        def finish(h):
-            o = sb.tile([P, 2, 2 * D], F32, name="o%d" % h)
-            for j in range(PACK):
-                u, c = divmod(j, 2)
+        def finish(h, first, last):
+            o = sb.tile([P, last - first, D], F32, name="o%d%d" % (h, first))
+            for j in range(first, last):
                 nc.vector.scalar_tensor_tensor(
-                    out=o[:, u, D * c : D * (c + 1)],
+                    out=o[:, j - first, :],
                     in0=y_banks[h % SIDE][:, j, :],
                     scalar=rstd[h][:, j : j + 1],
                     in1=gn_sb[:],
                     op0=ALU.mult,
                     op1=ALU.mult,
                 )
-            nc.sync.dma_start(out=out[h].rearrange("(u m c) e -> m u (c e)", u=2, c=2), in_=o[:])
+            nc.sync.dma_start(out=out[h].rearrange("(j m) e -> m j e", m=P)[:, first:last, :], in_=o[:])
 
-        group_q(0, 0)
-        quant_q(0, 0)
-        group_k(0, 0)
-        quant_k(0, 0)
-        group_k(0, 1)
-        group_q(0, 1)
-        quant_k(0, 1)
-        quant_q(0, 1)
-        group_k(1, 0)
-        group_k(1, 1)
-        quant_k(1, 0)
+        def part(h, src, j0, tiles):
+            first = P * (j0 - src)
+            weigh(h, j0, tiles, p_sb[h, src][:, :, first : first + P * tiles])
 
-        score_call(0, 0)
-        score_call(0, 1)
-        fills(0, 8)
+        front = []
+        def wide(h, r):
+            j0 = 1 if h < SIDE else 0
+            front.append(([("k", h // SIDE, r // 2), ("q", h // SIDE, j0), ("q", h // SIDE, 2)], ("p", h, j0, r), fill, (h, [r], j0, TILES - j0)))
+        def narrow(h):
+            front.append(([("k", 0, 0), ("k", 0, 1), ("q", 0, 0)], ("p", h, 0, 3), fill, (h, [0, 1, 2, 3], 0, 1)))
+        def vcopy(h):
+            front.append(([], ("vg", h), group_v, (h, nc.scalar.copy)))
+        def vals(h):
+            needs = [("w", h, 0), ("w", h, 2), ("v", h // 2)] + ([("w", h, 1)] if h < SIDE else [("o", h - SIDE)])
+            front.append((needs, ("y", h), values, (h, 0, TILES)))
+        def sq(h, a, b):
+            front.append(([], None, squares, (h, a, b)))
+        def rt(h):
+            front.append(([], ("r", h), root, (h,)))
+        taken = {SIDE * h + 3 * r: (h, r) for h in range(H) for r in range(PACK)}
+        for h in range(3):
+            narrow(h)
+        VAT = {18: 0, 21: 1, 24: 2, 27: 3, 32: 4, 35: 5, 36: 6}
+        for step in range(max(taken) + 1):
+            if step == 1:
+                narrow(3)
+            if step in VAT:
+                vcopy(VAT[step])
+            if step == 37:
+                vals(0)
+            if step in taken:
+                wide(*taken[step])
+        for h in range(1, SIDE):
+            vals(h)
+        sq(0, 0, 4)
+        for h in range(H - 1):
+            if h + 1 >= SIDE:
+                vals(h + 1)
+            if h == 1:
+                vcopy(7)
+            sq(h + 1, 0, 1)
+            rt(h)
+            sq(h + 1, 1, 4)
+        rt(7)
 
-        weigh(0)
-        quant_k(1, 1)
-        group_q(1, 0)
-        weigh(1)
-        quant_q(1, 0)
-        quant_w(0)
-        group_q(1, 1)
-        weigh(2)
-        quant_w(1)
-        quant_q(1, 1)
-        weigh(3)
-        quant_w(2)
+        back = []
+        def gk(s, a, raw, m0):
+            back.append(([], None, group_k, (s, a, raw, m0)))
+        def qk(s, a):
+            back.append(([], ("k", s, a), quant_k, (s, a)))
+        def gq(s, j0, tiles, raw):
+            back.append(([], None, group_q, (s, j0, tiles, raw)))
+        def qq(s, j0, tiles):
+            back.append(([], ("q", s, j0), quant_q, (s, j0, tiles)))
+        def wg(h, j0, tiles):
+            src = 0 if (h >= SIDE or j0 == 0) else 1
+            back.append(([("p", h, src, 3)], None, part, (h, src, j0, tiles)))
+        def qw(h, j0, tiles):
+            back.append(([], ("w", h, j0), quant_w, (h, j0, tiles)))
+        def qv(pair):
+            back.append(([("vg", 2 * pair), ("vg", 2 * pair + 1)], ("v", pair), quant_v, (pair,)))
+        def gv(h):
+            back.append(([], ("vg", h), group_v, (h, nc.vector.tensor_copy)))
+        def fin(h, a, b):
+            back.append(([("r", h)], ("o", h), finish, (h, a, b)))
 
-        fills(8, 16)
-        group_v(0, nc.scalar.copy)
-        group_v(1, nc.scalar.copy)
-        for n in range(4, 8):
-            weigh(n)
-            quant_w(n - 1)
-        quant_v(0)
-        quant_v(1)
+        for a in range(2):
+            gk(0, a, k0_low, 0)
+        for a in range(2):
+            gk(0, a, k0_high, P // 2)
+        gq(0, 0, 1, q0_first[:])
+        qk(0, 0)
+        qq(0, 0, 1)
+        qk(0, 1)
+        gq(0, 1, 1, q0_rest[:, :, 0:P])
+        gq(0, 2, 2, q0_rest[:, :, P:])
+        qq(0, 1, 1)
+        qq(0, 2, 2)
+        wg(0, 0, 1)
+        wg(1, 0, 1)
+        qw(0, 0, 1)
+        gk(1, 0, k1_raw, 0)
+        qw(1, 0, 1)
+        gk(1, 1, k1_raw, 0)
+        wg(2, 0, 1)
+        qk(1, 0)
+        wg(3, 0, 1)
+        qk(1, 1)
+        gq(1, 0, 2, q1_raw[:, :, 0 : 2 * P])
+        qw(2, 0, 1)
+        gq(1, 2, 2, q1_raw[:, :, 2 * P :])
+        qw(3, 0, 1)
+        qq(1, 0, 2)
+        qq(1, 2, 2)
+        parts = []
+        for h in range(H):
+            parts.extend([(h, 1, 1), (h, 2, 2)] if h < SIDE else [(h, 0, 2), (h, 2, 2)])
+        extra = {6: [(qv, (0,))], 10: [(qv, (1,))], 13: [(qv, (2,))], 14: [(fin, (0, 0, 4))], 15: [(fin, (1, 0, 4)), (fin, (2, 0, 4))]}
+        for n, item in enumerate(parts):
+            wg(*item)
+            if n > 0:
+                qw(*parts[n - 1])
+            for fn, args in extra.get(n, []):
+                fn(*args)
+        qv(3)
+        qw(*parts[-1])
+        for h in range(3, H - 1):
+            fin(h, 0, 4)
+        fin(7, 0, 2)
+        fin(7, 2, 4)
 
-        fills(16, 24)
-        for n in range(8, 12):
-            weigh(n)
-            quant_w(n - 1)
-
-        fills(24, 32)
-        for h in range(SIDE):
-            values(h, 0)
-            values(h, 1)
-
-        norm(0)
-        norm(1)
-        group_v(2, nc.scalar.copy)
-        norm(2)
-        norm(3)
-
-        weigh(12)
-        quant_w(11)
-        weigh(13)
-        quant_w(12)
-        group_v(3, nc.vector.tensor_copy)
-        finish(0)
-        weigh(14)
-        quant_w(13)
-        finish(1)
-        quant_v(2)
-        weigh(15)
-        quant_v(3)
-        quant_w(14)
-        finish(2)
-        quant_w(15)
-        finish(3)
-
-        for h in range(SIDE, H):
-            values(h, 0)
-            values(h, 1)
-            norm(h)
-            finish(h)
+        made = set()
+        queues = [front, back]
+        at = [0, 0]
+        while at[0] < len(front) or at[1] < len(back):
+            moved = False
+            for x in range(2):
+                while at[x] < len(queues[x]) and all(need in made for need in queues[x][at[x]][0]):
+                    needs, makes, fn, args = queues[x][at[x]]
+                    fn(*args)
+                    made.add(makes)
+                    at[x] = at[x] + 1
+                    moved = True
+            assert moved

@@ -18,7 +18,9 @@ PACK = 4
 SIDE = 4
 ROWS = P // SIDE
 TILES = NQ // P
-EPS = 1e-5 * 16.0 * 16.0
+RUN = 4
+EPS = 16.0 * 16.0 * 1e-5
+SKEW = 3
 
 
 def tile_rows_a_silu_kb_onorm_kernel(tc, qT, kT, t, v, kb, gn, out):
@@ -28,21 +30,15 @@ def tile_rows_a_silu_kb_onorm_kernel(tc, qT, kT, t, v, kb, gn, out):
         ps = ctx.enter_context(tc.psum_pool(name="ps", bufs=1))
         ctx.enter_context(tc.manual_schedule())
 
-        def quantize(name, grouped, words):
-            codes = sb.tile([P, words], U32, name=name + "_codes", align_bytes=64)
-            scales = sb.tile([P, words], U8, name=name + "_scales", align_bytes=64)
-            nc.vector.quantize_mx(out=codes[:].bitcast(FP8X4), scales=scales[:], in_=grouped)
-            return codes, scales
-
         def load_features(name, x, s, first, last):
             raw = sb.tile([P, PACK, last - first], F32, name=name)
-            src = x[SIDE * s : SIDE * (s + 1)].rearrange("h (p j) n -> (h p) j n", j=PACK)
+            src = x[SIDE * s : SIDE * (s + 1)].rearrange("h (m j) n -> (h m) j n", j=PACK)
             nc.sync.dma_start(out=raw[:], in_=src[:, :, first:last])
             return raw
 
-        def load_v(s):
+        def load_values(s):
             raw = sb.tile([P, SIDE, PACK * D], F32, name="v_raw%d" % s)
-            src = v[SIDE * s : SIDE * (s + 1)].rearrange("h (p j) e -> p h (j e)", j=PACK)
+            src = v[SIDE * s : SIDE * (s + 1)].rearrange("h (m r) e -> m h (r e)", r=PACK)
             nc.sync.dma_start(out=raw[:], in_=src)
             return raw
 
@@ -50,56 +46,54 @@ def tile_rows_a_silu_kb_onorm_kernel(tc, qT, kT, t, v, kb, gn, out):
         t_sb = sb.tile([P, PACK], F32)
         gn_sb = sb.tile([P, D], F32)
 
-        k0_low = load_features("k0_low", kT, 0, 0, N // 2)
-        k0_high = load_features("k0_high", kT, 0, N // 2, N)
-        q0_first = load_features("q0_first", qT, 0, 0, P)
-        nc.sync.dma_start(out=kb_sb[:], in_=kb.rearrange("(p j) o -> p (j o)", j=PACK))
-        nc.sync.dma_start(out=t_sb[:], in_=t.rearrange("(p j) o -> p (j o)", j=PACK))
-        q0_rest = load_features("q0_rest", qT, 0, P, NQ)
-        k1_raw = load_features("k1_raw", kT, 1, 0, N)
+        k_raw = [load_features("k_raw0", kT, 0, 0, N)]
+        q0_halves = [load_features("q0_low", qT, 0, 0, NQ // 2)]
+        nc.sync.dma_start(out=kb_sb[:], in_=kb.rearrange("(m r) o -> m (r o)", r=PACK))
+        nc.sync.dma_start(out=t_sb[:], in_=t.rearrange("(m r) o -> m (r o)", r=PACK))
+        q0_halves.append(load_features("q0_high", qT, 0, NQ // 2, NQ))
+        k_raw.append(load_features("k_raw1", kT, 1, 0, N))
         q1_raw = load_features("q1_raw", qT, 1, 0, NQ)
-        v_raw = [load_v(0), load_v(1)]
+        v_raw = [load_values(0), load_values(1)]
         nc.sync.dma_start(out=gn_sb[:], in_=gn)
 
-        grouped, q_mx, k_mx, v_mx, w_mx = {}, {}, {}, {}, {}
+        packed, mx, p_sb, sums, roots = {}, {}, {}, {}, {}
 
-        def group_q(s, j0, tiles, raw):
-            g = sb.tile([P, tiles * P * PACK], BF16, name="q_grp%d%d" % (s, j0), align_bytes=64)
-            grouped["q", s, j0] = g
+        def deal_four(key, raw, a):
+            packed[key] = sb.tile([P, 2 * P * PACK], BF16, name="%s%d%d" % key, align_bytes=64)
             nc.vector.tensor_copy(
-                out=g[:].rearrange("p (c i j) -> p c j i", i=2, j=PACK),
-                in_=raw.rearrange("p j (c i) -> p c j i", i=2),
-            )
-
-        def quant_q(s, j0, tiles):
-            mx = quantize("q%d%d" % (s, j0), grouped["q", s, j0][:], tiles * P)
-            for c in range(tiles):
-                q_mx[s, j0 + c] = (mx, slice(P * c, P * (c + 1)))
-
-        def group_k(s, a, raw, m0):
-            if m0 == 0:
-                grouped["k", s, a] = sb.tile([P, 2 * P * PACK], BF16, name="k_grp%d%d" % (s, a), align_bytes=64)
-            count = raw.shape[2] // PACK
-            nc.vector.tensor_copy(
-                out=grouped["k", s, a][:].rearrange("p (r m j) -> p m j r", r=2, j=PACK)[:, m0 : m0 + count],
+                out=packed[key][:].rearrange("p (r m j) -> p m j r", r=2, j=PACK),
                 in_=raw[:].rearrange("p j (m r) -> p m j r", r=PACK)[:, :, :, 2 * a : 2 * a + 2],
             )
 
-        def quant_k(s, a):
-            mx = quantize("k%d%d" % (s, a), grouped["k", s, a][:], 2 * P)
-            for r in range(2):
-                k_mx[s, 2 * a + r] = (mx, slice(P * r, P * (r + 1)))
-
-        def group_v(h, copy):
-            if h % 2 == 0:
-                grouped["v", h // 2] = sb.tile([P, 2, D * PACK], BF16, name="v_grp%d" % (h // 2), align_bytes=64)
-            copy(
-                out=grouped["v", h // 2][:, h % 2, :].rearrange("p (c i j) -> p c j i", i=2, j=PACK),
-                in_=v_raw[h // SIDE][:, h % SIDE, :].rearrange("p (j c i) -> p c j i", j=PACK, i=2),
+        def deal_two(key, raw):
+            packed[key] = sb.tile([P, 2 * P * PACK], BF16, name="%s%d%d" % key, align_bytes=64)
+            nc.vector.tensor_copy(
+                out=packed[key][:].rearrange("p (c m n j) -> p m j n c", c=2, n=2, j=PACK),
+                in_=raw[:].rearrange("p j (m n c) -> p m j n c", n=2, c=2),
             )
 
-        def quant_v(pair):
-            v_mx[pair] = quantize("v%d" % pair, grouped["v", pair][:].rearrange("p h x -> p (h x)"), 2 * D)
+        def pack_values(h, copy):
+            if h % 2 == 0:
+                packed["v", 0, h] = sb.tile([P, 2 * D * PACK], BF16, name="v%d" % h, align_bytes=64)
+            place = slice(D * PACK * (h % 2), D * PACK * (h % 2 + 1))
+            copy(
+                out=packed["v", 0, h - h % 2][:, place].rearrange("p (c i r) -> p c r i", i=RUN, r=PACK),
+                in_=v_raw[h // SIDE][:, h % SIDE, :].rearrange("p (r c i) -> p c r i", r=PACK, i=RUN),
+            )
+
+        def quantize(key, skip, tiles):
+            kind, group, first = key
+            name = "%s%d%d" % (kind, group, first + skip)
+            codes = sb.tile([P, tiles * P], U32, name=name + "_codes", align_bytes=64)
+            scales = sb.tile([P, tiles * P], U8, name=name + "_scales", align_bytes=64)
+            nc.vector.quantize_mx(
+                out=codes[:].bitcast(FP8X4),
+                scales=scales[:],
+                in_=packed[key][:, P * PACK * skip : P * PACK * (skip + tiles)],
+            )
+            for x in range(tiles):
+                cols = slice(P * x, P * (x + 1))
+                mx[kind, group, first + skip + x] = (codes[:, cols], scales[:, cols])
 
         score_banks = []
         y_banks = []
@@ -107,82 +101,74 @@ def tile_rows_a_silu_kb_onorm_kernel(tc, qT, kT, t, v, kb, gn, out):
             score_banks.append(ps.tile([P, PACK * P], F32, name="scores%d" % g))
             y_banks.append(ps.tile([P, TILES, D], F32, name="y%d" % g))
 
-        p_sb = {}
-
-        def fill(h, places, j0, tiles):
+        def scores(h, places, first, tiles):
             s, g = divmod(h, SIDE)
             rows = slice(ROWS * g, ROWS * (g + 1))
             width = tiles * P
             for x, r in enumerate(places):
-                k_tiles, kc = k_mx[s, r]
+                k_codes, k_scales = mx["k", s, r]
                 for c in range(tiles):
-                    q_tiles, qc = q_mx[s, j0 + c]
+                    q_codes, q_scales = mx["q", s, first + c]
                     nc.tensor.matmul_mx(
                         out=score_banks[g][:, width * x + P * c : width * x + P * (c + 1)],
-                        lhsT=k_tiles[0][rows, kc].bitcast(FP8X4),
-                        lhsT_scale=k_tiles[1][rows, kc],
-                        rhs=q_tiles[0][rows, qc].bitcast(FP8X4),
-                        rhs_scale=q_tiles[1][rows, qc],
+                        lhsT=k_codes[rows, :].bitcast(FP8X4),
+                        lhsT_scale=k_scales[rows, :],
+                        rhs=q_codes[rows, :].bitcast(FP8X4),
+                        rhs_scale=q_scales[rows, :],
                         start=True,
                         stop=True,
                     )
             if places[0] == 0:
-                p_sb[h, j0] = sb.tile([P, PACK, width], F32, name="p%d%d" % (h, j0))
+                p_sb[h, first] = sb.tile([P, PACK, width], F32, name="p%d%d" % (h, first))
             for x, r in enumerate(places):
                 nc.scalar.activation(
-                    out=p_sb[h, j0][:, r, :],
+                    out=p_sb[h, first][:, r, :],
                     in_=score_banks[g][:, width * x : width * (x + 1)],
                     func=ACT.Silu,
                     bias=kb_sb[:, r : r + 1],
                 )
 
-        def weigh(h, j0, tiles, p_part):
-            w = sb.tile([P, tiles * P * PACK], BF16, name="w_grp", tag="w_grp", bufs=3, align_bytes=64)
-            grouped["w", h, j0] = w
+        def weigh(h, p_first, first, tiles):
+            w = sb.tile([P, tiles * P * PACK], BF16, name="w", tag="w", bufs=3, align_bytes=64)
+            packed["w", h, first] = w
+            cols = slice(P * (first - p_first), P * (first - p_first + tiles))
             nc.vector.tensor_tensor(
-                out=w[:].rearrange("p (c i r) -> p c r i", i=2, r=PACK),
-                in0=p_part.rearrange("p r (c i) -> p c r i", i=2),
-                in1=t_sb[:].unsqueeze(1).unsqueeze(3).to_broadcast([P, tiles * P // 2, PACK, 2]),
+                out=w[:].rearrange("p (c i r) -> p c r i", i=RUN, r=PACK),
+                in0=p_sb[h, p_first][:, :, cols].rearrange("p r (c i) -> p c r i", i=RUN),
+                in1=t_sb[:].unsqueeze(1).unsqueeze(3).to_broadcast([P, tiles * P // RUN, PACK, RUN]),
                 op=ALU.mult,
             )
 
-        def quant_w(h, j0, tiles):
-            mx = quantize("w%d%d" % (h, j0), grouped["w", h, j0][:], tiles * P)
-            for c in range(tiles):
-                w_mx[h, j0 + c] = (mx, slice(P * c, P * (c + 1)))
-
-        def values(h, first, last):
-            vc = slice(D * (h % 2), D * (h % 2 + 1))
-            for j in range(first, last):
-                w_tiles, wc = w_mx[h, j]
+        def values(h):
+            v_codes, v_scales = mx["v", 0, h]
+            for j in range(TILES):
+                w_codes, w_scales = mx["w", h, j]
                 nc.tensor.matmul_mx(
                     out=y_banks[h % SIDE][:, j, :],
-                    lhsT=w_tiles[0][:, wc].bitcast(FP8X4),
-                    lhsT_scale=w_tiles[1][:, wc],
-                    rhs=v_mx[h // 2][0][:, vc].bitcast(FP8X4),
-                    rhs_scale=v_mx[h // 2][1][:, vc],
+                    lhsT=w_codes.bitcast(FP8X4),
+                    lhsT_scale=w_scales,
+                    rhs=v_codes.bitcast(FP8X4),
+                    rhs_scale=v_scales,
                     start=True,
                     stop=True,
                 )
 
-        ssq, rstd = {}, {}
-
         def squares(h, first, last):
             if first == 0:
-                ssq[h] = sb.tile([P, TILES], F32, name="ssq%d" % h)
+                sums[h] = sb.tile([P, TILES], F32, name="sums%d" % h)
             for j in range(first, last):
-                sq = sb.tile([P, D], F32, name="sq", tag="sq", bufs=4)
+                square = sb.tile([P, D], F32, name="square", tag="square", bufs=4)
                 nc.scalar.activation(
-                    out=sq[:],
+                    out=square[:],
                     in_=y_banks[h % SIDE][:, j, :],
                     func=ACT.Square,
-                    accum_out=ssq[h][:, j : j + 1],
+                    accum_out=sums[h][:, j : j + 1],
                 )
 
         def root(h):
-            rstd[h] = sb.tile([P, TILES], F32, name="rstd%d" % h)
+            roots[h] = sb.tile([P, TILES], F32, name="roots%d" % h)
             nc.scalar.activation(
-                out=rstd[h][:], in_=ssq[h][:], func=ACT.Abs_reciprocal_sqrt, scale=1.0 / D, bias=EPS
+                out=roots[h][:], in_=sums[h][:], func=ACT.Abs_reciprocal_sqrt, scale=1.0 / D, bias=EPS
             )
 
         def finish(h, first, last):
@@ -191,134 +177,142 @@ def tile_rows_a_silu_kb_onorm_kernel(tc, qT, kT, t, v, kb, gn, out):
                 nc.vector.scalar_tensor_tensor(
                     out=o[:, j - first, :],
                     in0=y_banks[h % SIDE][:, j, :],
-                    scalar=rstd[h][:, j : j + 1],
+                    scalar=roots[h][:, j : j + 1],
                     in1=gn_sb[:],
                     op0=ALU.mult,
                     op1=ALU.mult,
                 )
-            nc.sync.dma_start(out=out[h].rearrange("(j m) e -> m j e", m=P)[:, first:last, :], in_=o[:])
-
-        def part(h, src, j0, tiles):
-            first = P * (j0 - src)
-            weigh(h, j0, tiles, p_sb[h, src][:, :, first : first + P * tiles])
+            if h < SIDE:
+                nc.sync.dma_start(
+                    out=out[h].rearrange("(u m c) e -> m u (c e)", u=2, c=2),
+                    in_=o[:].rearrange("p (u c) e -> p u (c e)", c=2),
+                )
+            else:
+                nc.sync.dma_start(out=out[h].rearrange("(m c) e -> m c e", c=TILES)[:, first:last, :], in_=o[:])
 
         front = []
-        def wide(h, r):
-            j0 = 1 if h < SIDE else 0
-            front.append(([("k", h // SIDE, r // 2), ("q", h // SIDE, j0), ("q", h // SIDE, 2)], ("p", h, j0, r), fill, (h, [r], j0, TILES - j0)))
-        def narrow(h):
-            front.append(([("k", 0, 0), ("k", 0, 1), ("q", 0, 0)], ("p", h, 0, 3), fill, (h, [0, 1, 2, 3], 0, 1)))
-        def vcopy(h):
-            front.append(([], ("vg", h), group_v, (h, nc.scalar.copy)))
-        def vals(h):
-            needs = [("w", h, 0), ("w", h, 2), ("v", h // 2)] + ([("w", h, 1)] if h < SIDE else [("o", h - SIDE)])
-            front.append((needs, ("y", h), values, (h, 0, TILES)))
-        def sq(h, a, b):
-            front.append(([], None, squares, (h, a, b)))
-        def rt(h):
-            front.append(([], ("r", h), root, (h,)))
-        taken = {SIDE * h + 3 * r: (h, r) for h in range(H) for r in range(PACK)}
-        for h in range(3):
-            narrow(h)
-        VAT = {18: 0, 21: 1, 24: 2, 27: 3, 32: 4, 35: 5, 36: 6}
-        for step in range(max(taken) + 1):
-            if step == 1:
-                narrow(3)
-            if step in VAT:
-                vcopy(VAT[step])
-            if step == 37:
-                vals(0)
-            if step in taken:
-                wide(*taken[step])
-        for h in range(1, SIDE):
-            vals(h)
-        sq(0, 0, 4)
-        for h in range(H - 1):
-            if h + 1 >= SIDE:
-                vals(h + 1)
-            if h == 1:
-                vcopy(7)
-            sq(h + 1, 0, 1)
-            rt(h)
-            sq(h + 1, 1, 4)
-        rt(7)
-
         back = []
-        def gk(s, a, raw, m0):
-            back.append(([], None, group_k, (s, a, raw, m0)))
-        def qk(s, a):
-            back.append(([], ("k", s, a), quant_k, (s, a)))
-        def gq(s, j0, tiles, raw):
-            back.append(([], None, group_q, (s, j0, tiles, raw)))
-        def qq(s, j0, tiles):
-            back.append(([], ("q", s, j0), quant_q, (s, j0, tiles)))
-        def wg(h, j0, tiles):
-            src = 0 if (h >= SIDE or j0 == 0) else 1
-            back.append(([("p", h, src, 3)], None, part, (h, src, j0, tiles)))
-        def qw(h, j0, tiles):
-            back.append(([], ("w", h, j0), quant_w, (h, j0, tiles)))
-        def qv(pair):
-            back.append(([("vg", 2 * pair), ("vg", 2 * pair + 1)], ("v", pair), quant_v, (pair,)))
-        def gv(h):
-            back.append(([], ("vg", h), group_v, (h, nc.vector.tensor_copy)))
-        def fin(h, a, b):
-            back.append(([("r", h)], ("o", h), finish, (h, a, b)))
+
+        def add_scores(h, places, first, tiles):
+            s = h // SIDE
+            needs = [("k", s, r) for r in places] + [("q", s, first + c) for c in range(tiles)]
+            front.append((needs, [("p", h, first, places[-1])], scores, (h, places, first, tiles)))
+
+        def add_values(h):
+            needs = [("w", h, j) for j in range(TILES)] + [("v", 0, h)]
+            if h >= SIDE:
+                needs.append(("out", h - SIDE))
+            front.append((needs, [], values, (h,)))
+
+        def add_quantize(key, skip, tiles, needs):
+            makes = [(key[0], key[1], key[2] + skip + x) for x in range(tiles)]
+            back.append((needs, makes, quantize, (key, skip, tiles)))
+
+        def add_weigh(h, p_first, first, tiles):
+            back.append(([("p", h, p_first, PACK - 1)], [], weigh, (h, p_first, first, tiles)))
+
+        def add_quantize_values(h):
+            add_quantize(("v", 0, h), 0, 2, [("packed v", h), ("packed v", h + 1)])
+
+        def add_finish(h, first, last):
+            back.append(([("root", h)], [("out", h)], finish, (h, first, last)))
+
+        grid = {SIDE * h + SKEW * r: (h, r) for h in range(H) for r in range(PACK)}
+        last_step = max(grid)
+        for h in range(SIDE - 1):
+            add_scores(h, [0, 1, 2, 3], 0, 1)
+        scalar_packs = 0
+        for step in range(last_step + 1):
+            if step in grid:
+                h, r = grid[step]
+                if step == last_step:
+                    add_values(0)
+                    front.append(([], [], squares, (0, 0, TILES)))
+                first = 1 if h < SIDE else 0
+                add_scores(h, [r], first, TILES - first)
+            elif step == 1:
+                add_scores(SIDE - 1, [0, 1, 2, 3], 0, 1)
+            head_done = step in grid and grid[step][1] == PACK - 1 and 2 <= grid[step][0] <= 5
+            gap_opens = step > last_step // 2 and step in grid and step + 1 not in grid and step < last_step
+            if head_done or gap_opens:
+                front.append(([], [("packed v", scalar_packs)], pack_values, (scalar_packs, nc.scalar.copy)))
+                scalar_packs = scalar_packs + 1
+        for h in range(1, SIDE):
+            add_values(h)
+        front.append(([], [("root", 0)], root, (0,)))
+        front.append(([], [], squares, (1, 0, TILES)))
+        for h in range(1, H - 1):
+            if h + 1 >= SIDE:
+                add_values(h + 1)
+            front.append(([], [], squares, (h + 1, 0, 1)))
+            front.append(([], [("root", h)], root, (h,)))
+            front.append(([], [], squares, (h + 1, 1, TILES)))
+        front.append(([], [("root", H - 1)], root, (H - 1,)))
 
         for a in range(2):
-            gk(0, a, k0_low, 0)
-        for a in range(2):
-            gk(0, a, k0_high, P // 2)
-        gq(0, 0, 1, q0_first[:])
-        qk(0, 0)
-        qq(0, 0, 1)
-        qk(0, 1)
-        gq(0, 1, 1, q0_rest[:, :, 0:P])
-        gq(0, 2, 2, q0_rest[:, :, P:])
-        qq(0, 1, 1)
-        qq(0, 2, 2)
-        wg(0, 0, 1)
-        wg(1, 0, 1)
-        qw(0, 0, 1)
-        gk(1, 0, k1_raw, 0)
-        qw(1, 0, 1)
-        gk(1, 1, k1_raw, 0)
-        wg(2, 0, 1)
-        qk(1, 0)
-        wg(3, 0, 1)
-        qk(1, 1)
-        gq(1, 0, 2, q1_raw[:, :, 0 : 2 * P])
-        qw(2, 0, 1)
-        gq(1, 2, 2, q1_raw[:, :, 2 * P :])
-        qw(3, 0, 1)
-        qq(1, 0, 2)
-        qq(1, 2, 2)
-        parts = []
-        for h in range(H):
-            parts.extend([(h, 1, 1), (h, 2, 2)] if h < SIDE else [(h, 0, 2), (h, 2, 2)])
-        extra = {6: [(qv, (0,))], 10: [(qv, (1,))], 13: [(qv, (2,))], 14: [(fin, (0, 0, 4))], 15: [(fin, (1, 0, 4)), (fin, (2, 0, 4))]}
-        for n, item in enumerate(parts):
-            wg(*item)
-            if n > 0:
-                qw(*parts[n - 1])
-            for fn, args in extra.get(n, []):
-                fn(*args)
-        qv(3)
-        qw(*parts[-1])
-        for h in range(3, H - 1):
-            fin(h, 0, 4)
-        fin(7, 0, 2)
-        fin(7, 2, 4)
+            back.append(([], [], deal_four, (("k", 0, 2 * a), k_raw[0], a)))
+        add_quantize(("k", 0, 0), 0, 2, [])
+        back.append(([], [], deal_two, (("q", 0, 0), q0_halves[0])))
+        add_quantize(("k", 0, 2), 0, 2, [])
+        add_quantize(("q", 0, 0), 0, 2, [])
+        back.append(([], [], deal_two, (("q", 0, 2), q0_halves[1])))
+        add_quantize(("q", 0, 2), 0, 2, [])
+        add_weigh(0, 0, 0, 1)
+        back.append(([], [], deal_four, (("k", 1, 0), k_raw[1], 0)))
+        add_quantize(("w", 0, 0), 0, 1, [])
+        add_weigh(1, 0, 0, 1)
+        back.append(([], [], deal_four, (("k", 1, 2), k_raw[1], 1)))
+        add_quantize(("w", 1, 0), 0, 1, [])
+        add_weigh(2, 0, 0, 1)
+        add_quantize(("k", 1, 0), 0, 2, [])
+        add_weigh(3, 0, 0, 1)
+        add_quantize(("w", 2, 0), 0, 1, [])
+        add_quantize(("k", 1, 2), 0, 2, [])
+        back.append(([], [], deal_four, (("q", 1, 0), q1_raw, 0)))
+        add_quantize(("w", 3, 0), 0, 1, [])
+        back.append(([], [], deal_four, (("q", 1, 2), q1_raw, 1)))
+        add_quantize(("q", 1, 0), 0, 2, [])
+        add_quantize(("q", 1, 2), 0, 2, [])
+        add_weigh(0, 1, 1, 3)
+        for h in range(1, SIDE):
+            add_weigh(h, 1, 1, 3)
+            add_quantize(("w", h - 1, 1), 0, 1, [])
+            add_quantize(("w", h - 1, 1), 1, 2, [])
+        for h in range(H - 2, H):
+            back.append(([], [("packed v", h)], pack_values, (h, nc.vector.tensor_copy)))
+        add_quantize(("w", 3, 1), 0, 1, [])
+        add_quantize(("w", 3, 1), 1, 2, [])
+        add_quantize_values(0)
+        add_quantize_values(6)
+        add_weigh(4, 0, 0, 4)
+        add_weigh(5, 0, 0, 4)
+        add_quantize(("w", 4, 0), 0, 4, [])
+        add_quantize_values(2)
+        add_weigh(6, 0, 0, 4)
+        add_quantize(("w", 5, 0), 0, 4, [])
+        add_quantize_values(4)
+        add_weigh(7, 0, 0, 2)
+        add_quantize(("w", 6, 0), 0, 4, [])
+        add_finish(0, 0, TILES)
+        add_finish(1, 0, TILES)
+        add_quantize(("w", 7, 0), 0, 2, [])
+        add_finish(2, 0, TILES)
+        add_weigh(7, 0, 2, 2)
+        add_finish(3, 0, TILES)
+        add_quantize(("w", 7, 2), 0, 2, [])
+        for h in range(SIDE, H - 1):
+            add_finish(h, 0, TILES)
+        add_finish(H - 1, 0, 2)
+        add_finish(H - 1, 2, TILES)
 
         made = set()
-        queues = [front, back]
-        at = [0, 0]
-        while at[0] < len(front) or at[1] < len(back):
-            moved = False
-            for x in range(2):
-                while at[x] < len(queues[x]) and all(need in made for need in queues[x][at[x]][0]):
-                    needs, makes, fn, args = queues[x][at[x]]
-                    fn(*args)
-                    made.add(makes)
-                    at[x] = at[x] + 1
-                    moved = True
-            assert moved
+        programs = [front, back]
+        done = [0, 0]
+        while done[0] < len(front) or done[1] < len(back):
+            for x, program in enumerate(programs):
+                while done[x] < len(program) and all(need in made for need in program[done[x]][0]):
+                    needs, makes, call, args = program[done[x]]
+                    call(*args)
+                    for key in makes:
+                        made.add(key)
+                    done[x] = done[x] + 1

@@ -46,9 +46,9 @@ def tile_rows_a_silu_kb_onorm_kernel(tc, qT, kT, t, v, kb, gn, out):
         t_sb = sb.tile([P, PACK], F32)
         gn_sb = sb.tile([P, D], F32)
 
+        nc.scalar.dma_start(out=kb_sb[:], in_=kb.rearrange("(m r) o -> m (r o)", r=PACK))
         k_raw = [load_features("k_raw0", kT, 0, 0, N)]
         q0_halves = [load_features("q0_low", qT, 0, 0, NQ // 2)]
-        nc.sync.dma_start(out=kb_sb[:], in_=kb.rearrange("(m r) o -> m (r o)", r=PACK))
         nc.sync.dma_start(out=t_sb[:], in_=t.rearrange("(m r) o -> m (r o)", r=PACK))
         q0_halves.append(load_features("q0_high", qT, 0, NQ // 2, NQ))
         k_raw.append(load_features("k_raw1", kT, 1, 0, N))
@@ -58,9 +58,9 @@ def tile_rows_a_silu_kb_onorm_kernel(tc, qT, kT, t, v, kb, gn, out):
 
         packed, mx, p_sb, sums, roots = {}, {}, {}, {}, {}
 
-        def deal_four(key, raw, a):
+        def deal_four(key, raw, a, copy):
             packed[key] = sb.tile([P, 2 * P * PACK], BF16, name="%s%d%d" % key, align_bytes=64)
-            nc.vector.tensor_copy(
+            copy(
                 out=packed[key][:].rearrange("p (r m j) -> p m j r", r=2, j=PACK),
                 in_=raw[:].rearrange("p j (m r) -> p m j r", r=PACK)[:, :, :, 2 * a : 2 * a + 2],
             )
@@ -73,8 +73,8 @@ def tile_rows_a_silu_kb_onorm_kernel(tc, qT, kT, t, v, kb, gn, out):
             )
 
         def pack_values(h, copy):
-            if h % 2 == 0:
-                packed["v", 0, h] = sb.tile([P, 2 * D * PACK], BF16, name="v%d" % h, align_bytes=64)
+            if ("v", 0, h - h % 2) not in packed:
+                packed["v", 0, h - h % 2] = sb.tile([P, 2 * D * PACK], BF16, name="v%d" % h, align_bytes=64)
             place = slice(D * PACK * (h % 2), D * PACK * (h % 2 + 1))
             copy(
                 out=packed["v", 0, h - h % 2][:, place].rearrange("p (c i r) -> p c r i", i=RUN, r=PACK),
@@ -165,10 +165,14 @@ def tile_rows_a_silu_kb_onorm_kernel(tc, qT, kT, t, v, kb, gn, out):
                     accum_out=sums[h][:, j : j + 1],
                 )
 
-        def root(h):
-            roots[h] = sb.tile([P, TILES], F32, name="roots%d" % h)
+        def root(h, first, last):
+            roots[h, first] = sb.tile([P, last - first], F32, name="roots%d%d" % (h, first))
             nc.scalar.activation(
-                out=roots[h][:], in_=sums[h][:], func=ACT.Abs_reciprocal_sqrt, scale=1.0 / D, bias=EPS
+                out=roots[h, first][:],
+                in_=sums[h][:, first:last],
+                func=ACT.Abs_reciprocal_sqrt,
+                scale=1.0 / D,
+                bias=EPS,
             )
 
         def finish(h, first, last):
@@ -177,7 +181,7 @@ def tile_rows_a_silu_kb_onorm_kernel(tc, qT, kT, t, v, kb, gn, out):
                 nc.vector.scalar_tensor_tensor(
                     out=o[:, j - first, :],
                     in0=y_banks[h % SIDE][:, j, :],
-                    scalar=roots[h][:, j : j + 1],
+                    scalar=roots[h, first][:, j - first : j - first + 1],
                     in1=gn_sb[:],
                     op0=ALU.mult,
                     op1=ALU.mult,
@@ -201,8 +205,14 @@ def tile_rows_a_silu_kb_onorm_kernel(tc, qT, kT, t, v, kb, gn, out):
         def add_values(h):
             needs = [("w", h, j) for j in range(TILES)] + [("v", 0, h)]
             if h >= SIDE:
-                needs.append(("out", h - SIDE))
+                needs.append(("out", h - SIDE, 0))
             front.append((needs, [], values, (h,)))
+
+        def add_squares(h, first, last):
+            front.append(([], [], squares, (h, first, last)))
+
+        def add_root(h, first, last):
+            front.append(([], [("root", h, first)], root, (h, first, last)))
 
         def add_quantize(key, skip, tiles, needs):
             makes = [(key[0], key[1], key[2] + skip + x) for x in range(tiles)]
@@ -215,10 +225,11 @@ def tile_rows_a_silu_kb_onorm_kernel(tc, qT, kT, t, v, kb, gn, out):
             add_quantize(("v", 0, h), 0, 2, [("packed v", h), ("packed v", h + 1)])
 
         def add_finish(h, first, last):
-            back.append(([("root", h)], [("out", h)], finish, (h, first, last)))
+            back.append(([("root", h, first)], [("out", h, first)], finish, (h, first, last)))
 
         grid = {SIDE * h + SKEW * r: (h, r) for h in range(H) for r in range(PACK)}
         last_step = max(grid)
+        front.append(([], [("packed k",)], deal_four, (("k", 0, 2), k_raw[0], 1, nc.scalar.copy)))
         for h in range(SIDE - 1):
             add_scores(h, [0, 1, 2, 3], 0, 1)
         scalar_packs = 0
@@ -227,7 +238,7 @@ def tile_rows_a_silu_kb_onorm_kernel(tc, qT, kT, t, v, kb, gn, out):
                 h, r = grid[step]
                 if step == last_step:
                     add_values(0)
-                    front.append(([], [], squares, (0, 0, TILES)))
+                    add_squares(0, 0, TILES)
                 first = 1 if h < SIDE else 0
                 add_scores(h, [r], first, TILES - first)
             elif step == 1:
@@ -239,38 +250,46 @@ def tile_rows_a_silu_kb_onorm_kernel(tc, qT, kT, t, v, kb, gn, out):
                 scalar_packs = scalar_packs + 1
         for h in range(1, SIDE):
             add_values(h)
-        front.append(([], [("root", 0)], root, (0,)))
-        front.append(([], [], squares, (1, 0, TILES)))
-        for h in range(1, H - 1):
+        add_root(0, 0, TILES)
+        add_squares(1, 0, TILES)
+        front.append(([], [("packed v", 6)], pack_values, (6, nc.scalar.copy)))
+        add_root(1, 0, TILES)
+        add_squares(2, 0, TILES)
+        for h in range(2, H - 2):
             if h + 1 >= SIDE:
                 add_values(h + 1)
-            front.append(([], [], squares, (h + 1, 0, 1)))
-            front.append(([], [("root", h)], root, (h,)))
-            front.append(([], [], squares, (h + 1, 1, TILES)))
-        front.append(([], [("root", H - 1)], root, (H - 1,)))
+            add_squares(h + 1, 0, 1)
+            add_root(h, 0, TILES)
+            add_squares(h + 1, 1, TILES)
+        add_root(H - 2, 0, TILES)
+        add_values(H - 1)
+        add_squares(H - 1, 0, 3)
+        add_root(H - 1, 0, 2)
+        add_squares(H - 1, 3, TILES)
+        add_root(H - 1, 2, TILES)
 
-        for a in range(2):
-            back.append(([], [], deal_four, (("k", 0, 2 * a), k_raw[0], a)))
+        back.append(([], [], deal_four, (("k", 0, 0), k_raw[0], 0, nc.vector.tensor_copy)))
         add_quantize(("k", 0, 0), 0, 2, [])
         back.append(([], [], deal_two, (("q", 0, 0), q0_halves[0])))
-        add_quantize(("k", 0, 2), 0, 2, [])
-        add_quantize(("q", 0, 0), 0, 2, [])
+        add_quantize(("k", 0, 2), 0, 2, [("packed k",)])
+        add_quantize(("q", 0, 0), 0, 1, [])
+        add_quantize(("q", 0, 0), 1, 1, [])
         back.append(([], [], deal_two, (("q", 0, 2), q0_halves[1])))
         add_quantize(("q", 0, 2), 0, 2, [])
         add_weigh(0, 0, 0, 1)
-        back.append(([], [], deal_four, (("k", 1, 0), k_raw[1], 0)))
+        back.append(([], [], deal_four, (("k", 1, 0), k_raw[1], 0, nc.vector.tensor_copy)))
         add_quantize(("w", 0, 0), 0, 1, [])
         add_weigh(1, 0, 0, 1)
-        back.append(([], [], deal_four, (("k", 1, 2), k_raw[1], 1)))
+        back.append(([], [], deal_four, (("k", 1, 2), k_raw[1], 1, nc.vector.tensor_copy)))
         add_quantize(("w", 1, 0), 0, 1, [])
         add_weigh(2, 0, 0, 1)
         add_quantize(("k", 1, 0), 0, 2, [])
         add_weigh(3, 0, 0, 1)
         add_quantize(("w", 2, 0), 0, 1, [])
         add_quantize(("k", 1, 2), 0, 2, [])
-        back.append(([], [], deal_four, (("q", 1, 0), q1_raw, 0)))
+        back.append(([], [], deal_four, (("q", 1, 0), q1_raw, 0, nc.vector.tensor_copy)))
         add_quantize(("w", 3, 0), 0, 1, [])
-        back.append(([], [], deal_four, (("q", 1, 2), q1_raw, 1)))
+        back.append(([], [], deal_four, (("q", 1, 2), q1_raw, 1, nc.vector.tensor_copy)))
         add_quantize(("q", 1, 0), 0, 2, [])
         add_quantize(("q", 1, 2), 0, 2, [])
         add_weigh(0, 1, 1, 3)
@@ -278,12 +297,10 @@ def tile_rows_a_silu_kb_onorm_kernel(tc, qT, kT, t, v, kb, gn, out):
             add_weigh(h, 1, 1, 3)
             add_quantize(("w", h - 1, 1), 0, 1, [])
             add_quantize(("w", h - 1, 1), 1, 2, [])
-        for h in range(H - 2, H):
-            back.append(([], [("packed v", h)], pack_values, (h, nc.vector.tensor_copy)))
+        back.append(([], [("packed v", 7)], pack_values, (7, nc.vector.tensor_copy)))
         add_quantize(("w", 3, 1), 0, 1, [])
         add_quantize(("w", 3, 1), 1, 2, [])
         add_quantize_values(0)
-        add_quantize_values(6)
         add_weigh(4, 0, 0, 4)
         add_weigh(5, 0, 0, 4)
         add_quantize(("w", 4, 0), 0, 4, [])
@@ -297,6 +314,7 @@ def tile_rows_a_silu_kb_onorm_kernel(tc, qT, kT, t, v, kb, gn, out):
         add_finish(1, 0, TILES)
         add_quantize(("w", 7, 0), 0, 2, [])
         add_finish(2, 0, TILES)
+        add_quantize_values(6)
         add_weigh(7, 0, 2, 2)
         add_finish(3, 0, TILES)
         add_quantize(("w", 7, 2), 0, 2, [])

@@ -21,6 +21,7 @@ TILES = NQ // P
 RUN = 4
 EPS = 16.0 * 16.0 * 1e-5
 SKEW = 3
+SCALAR_PACKS = range(1, 6)
 
 
 def tile_rows_a_silu_kb_onorm_kernel(tc, qT, kT, t, v, kb, gn, out):
@@ -73,11 +74,11 @@ def tile_rows_a_silu_kb_onorm_kernel(tc, qT, kT, t, v, kb, gn, out):
             )
 
         def pack_values(h, copy):
-            if ("v", 0, h - h % 2) not in packed:
-                packed["v", 0, h - h % 2] = sb.tile([P, 2 * D * PACK], BF16, name="v%d" % h, align_bytes=64)
-            place = slice(D * PACK * (h % 2), D * PACK * (h % 2 + 1))
+            if h % 2 == 0:
+                packed["v", 0, h] = sb.tile([P, 2 * D * PACK], BF16, name="v%d" % h, align_bytes=64)
+            cols = slice(D * PACK * (h % 2), D * PACK * (h % 2 + 1))
             copy(
-                out=packed["v", 0, h - h % 2][:, place].rearrange("p (c i r) -> p c r i", i=RUN, r=PACK),
+                out=packed["v", 0, h - h % 2][:, cols].rearrange("p (c i r) -> p c r i", i=RUN, r=PACK),
                 in_=v_raw[h // SIDE][:, h % SIDE, :].rearrange("p (r c i) -> p c r i", r=PACK, i=RUN),
             )
 
@@ -214,25 +215,36 @@ def tile_rows_a_silu_kb_onorm_kernel(tc, qT, kT, t, v, kb, gn, out):
         def add_root(h, first, last):
             front.append(([], [("root", h, first)], root, (h, first, last)))
 
+        def add_pack(program, h, copy):
+            needs = [("packed v", h - 1)] if h % 2 else []
+            program.append((needs, [("packed v", h)], pack_values, (h, copy)))
+
+        def add_deal(key, raw, a):
+            back.append(([], [], deal_four, (key, raw, a, nc.vector.tensor_copy)))
+
         def add_quantize(key, skip, tiles, needs):
             makes = [(key[0], key[1], key[2] + skip + x) for x in range(tiles)]
             back.append((needs, makes, quantize, (key, skip, tiles)))
 
-        def add_weigh(h, p_first, first, tiles):
-            back.append(([("p", h, p_first, PACK - 1)], [], weigh, (h, p_first, first, tiles)))
-
         def add_quantize_values(h):
             add_quantize(("v", 0, h), 0, 2, [("packed v", h), ("packed v", h + 1)])
+
+        def add_quantize_three(h):
+            add_quantize(("w", h, 1), 0, 1, [])
+            add_quantize(("w", h, 1), 1, 2, [])
+
+        def add_weigh(h, p_first, first, tiles):
+            back.append(([("p", h, p_first, PACK - 1)], [], weigh, (h, p_first, first, tiles)))
 
         def add_finish(h, first, last):
             back.append(([("root", h, first)], [("out", h, first)], finish, (h, first, last)))
 
+        front.append(([], [("packed k",)], deal_four, (("k", 0, 2), k_raw[0], 1, nc.scalar.copy)))
         grid = {SIDE * h + SKEW * r: (h, r) for h in range(H) for r in range(PACK)}
         last_step = max(grid)
-        front.append(([], [("packed k",)], deal_four, (("k", 0, 2), k_raw[0], 1, nc.scalar.copy)))
         for h in range(SIDE - 1):
-            add_scores(h, [0, 1, 2, 3], 0, 1)
-        scalar_packs = 0
+            add_scores(h, list(range(PACK)), 0, 1)
+        next_pack = SCALAR_PACKS.start
         for step in range(last_step + 1):
             if step in grid:
                 h, r = grid[step]
@@ -241,34 +253,29 @@ def tile_rows_a_silu_kb_onorm_kernel(tc, qT, kT, t, v, kb, gn, out):
                     add_squares(0, 0, TILES)
                 first = 1 if h < SIDE else 0
                 add_scores(h, [r], first, TILES - first)
+                head_done = r == PACK - 1 and 3 <= h <= 5
+                gap_opens = h == H - 1 and step + 1 not in grid and step < last_step
+                if head_done or gap_opens:
+                    add_pack(front, next_pack, nc.scalar.copy)
+                    next_pack = next_pack + 1
             elif step == 1:
-                add_scores(SIDE - 1, [0, 1, 2, 3], 0, 1)
-            head_done = step in grid and grid[step][1] == PACK - 1 and 2 <= grid[step][0] <= 5
-            gap_opens = step > last_step // 2 and step in grid and step + 1 not in grid and step < last_step
-            if head_done or gap_opens:
-                front.append(([], [("packed v", scalar_packs)], pack_values, (scalar_packs, nc.scalar.copy)))
-                scalar_packs = scalar_packs + 1
+                add_scores(SIDE - 1, list(range(PACK)), 0, 1)
+        assert next_pack == SCALAR_PACKS.stop
         for h in range(1, SIDE):
             add_values(h)
         add_root(0, 0, TILES)
         add_squares(1, 0, TILES)
-        front.append(([], [("packed v", 6)], pack_values, (6, nc.scalar.copy)))
-        add_root(1, 0, TILES)
-        add_squares(2, 0, TILES)
-        for h in range(2, H - 2):
+        for h in range(1, H - 1):
             if h + 1 >= SIDE:
                 add_values(h + 1)
             add_squares(h + 1, 0, 1)
             add_root(h, 0, TILES)
-            add_squares(h + 1, 1, TILES)
-        add_root(H - 2, 0, TILES)
-        add_values(H - 1)
-        add_squares(H - 1, 0, 3)
-        add_root(H - 1, 0, 2)
-        add_squares(H - 1, 3, TILES)
-        add_root(H - 1, 2, TILES)
+            add_squares(h + 1, 1, TILES if h + 1 < H - 1 else TILES - 1)
+        add_root(H - 1, 0, TILES // 2)
+        add_squares(H - 1, TILES - 1, TILES)
+        add_root(H - 1, TILES // 2, TILES)
 
-        back.append(([], [], deal_four, (("k", 0, 0), k_raw[0], 0, nc.vector.tensor_copy)))
+        add_deal(("k", 0, 0), k_raw[0], 0)
         add_quantize(("k", 0, 0), 0, 2, [])
         back.append(([], [], deal_two, (("q", 0, 0), q0_halves[0])))
         add_quantize(("k", 0, 2), 0, 2, [("packed k",)])
@@ -277,51 +284,50 @@ def tile_rows_a_silu_kb_onorm_kernel(tc, qT, kT, t, v, kb, gn, out):
         back.append(([], [], deal_two, (("q", 0, 2), q0_halves[1])))
         add_quantize(("q", 0, 2), 0, 2, [])
         add_weigh(0, 0, 0, 1)
-        back.append(([], [], deal_four, (("k", 1, 0), k_raw[1], 0, nc.vector.tensor_copy)))
+        add_deal(("k", 1, 0), k_raw[1], 0)
         add_quantize(("w", 0, 0), 0, 1, [])
         add_weigh(1, 0, 0, 1)
-        back.append(([], [], deal_four, (("k", 1, 2), k_raw[1], 1, nc.vector.tensor_copy)))
+        add_deal(("k", 1, 2), k_raw[1], 1)
         add_quantize(("w", 1, 0), 0, 1, [])
         add_weigh(2, 0, 0, 1)
         add_quantize(("k", 1, 0), 0, 2, [])
         add_weigh(3, 0, 0, 1)
         add_quantize(("w", 2, 0), 0, 1, [])
         add_quantize(("k", 1, 2), 0, 2, [])
-        back.append(([], [], deal_four, (("q", 1, 0), q1_raw, 0, nc.vector.tensor_copy)))
+        add_deal(("q", 1, 0), q1_raw, 0)
         add_quantize(("w", 3, 0), 0, 1, [])
-        back.append(([], [], deal_four, (("q", 1, 2), q1_raw, 1, nc.vector.tensor_copy)))
+        add_deal(("q", 1, 2), q1_raw, 1)
         add_quantize(("q", 1, 0), 0, 2, [])
         add_quantize(("q", 1, 2), 0, 2, [])
-        add_weigh(0, 1, 1, 3)
+        for h in range(SCALAR_PACKS.start):
+            add_pack(back, h, nc.vector.tensor_copy)
+        add_weigh(0, 1, 1, TILES - 1)
         for h in range(1, SIDE):
-            add_weigh(h, 1, 1, 3)
-            add_quantize(("w", h - 1, 1), 0, 1, [])
-            add_quantize(("w", h - 1, 1), 1, 2, [])
-        back.append(([], [("packed v", 7)], pack_values, (7, nc.vector.tensor_copy)))
-        add_quantize(("w", 3, 1), 0, 1, [])
-        add_quantize(("w", 3, 1), 1, 2, [])
+            add_weigh(h, 1, 1, TILES - 1)
+            add_quantize_three(h - 1)
+        for h in range(SCALAR_PACKS.stop, H):
+            add_pack(back, h, nc.vector.tensor_copy)
+        add_quantize_three(SIDE - 1)
         add_quantize_values(0)
-        add_weigh(4, 0, 0, 4)
-        add_weigh(5, 0, 0, 4)
-        add_quantize(("w", 4, 0), 0, 4, [])
-        add_quantize_values(2)
-        add_weigh(6, 0, 0, 4)
-        add_quantize(("w", 5, 0), 0, 4, [])
-        add_quantize_values(4)
-        add_weigh(7, 0, 0, 2)
-        add_quantize(("w", 6, 0), 0, 4, [])
+        add_quantize_values(6)
+        add_weigh(4, 0, 0, TILES)
+        for h in range(5, H - 1):
+            add_weigh(h, 0, 0, TILES)
+            add_quantize(("w", h - 1, 0), 0, TILES, [])
+            add_quantize_values(2 * (h - SIDE))
+        add_weigh(H - 1, 0, 0, 2)
+        add_quantize(("w", H - 2, 0), 0, TILES, [])
         add_finish(0, 0, TILES)
         add_finish(1, 0, TILES)
-        add_quantize(("w", 7, 0), 0, 2, [])
+        add_quantize(("w", H - 1, 0), 0, 2, [])
         add_finish(2, 0, TILES)
-        add_quantize_values(6)
-        add_weigh(7, 0, 2, 2)
+        add_weigh(H - 1, 0, 2, 2)
         add_finish(3, 0, TILES)
-        add_quantize(("w", 7, 2), 0, 2, [])
+        add_quantize(("w", H - 1, 2), 0, 2, [])
         for h in range(SIDE, H - 1):
             add_finish(h, 0, TILES)
-        add_finish(H - 1, 0, 2)
-        add_finish(H - 1, 2, TILES)
+        add_finish(H - 1, 0, TILES // 2)
+        add_finish(H - 1, TILES // 2, TILES)
 
         made = set()
         programs = [front, back]
@@ -329,8 +335,8 @@ def tile_rows_a_silu_kb_onorm_kernel(tc, qT, kT, t, v, kb, gn, out):
         while done[0] < len(front) or done[1] < len(back):
             for x, program in enumerate(programs):
                 while done[x] < len(program) and all(need in made for need in program[done[x]][0]):
-                    needs, makes, call, args = program[done[x]]
-                    call(*args)
-                    for key in makes:
+                    entry = program[done[x]]
+                    entry[2](*entry[3])
+                    for key in entry[1]:
                         made.add(key)
                     done[x] = done[x] + 1

from contextlib import ExitStack

import concourse.mybir as mybir

H, D, NQ, N = 8, 128, 512, 512
FLOPS = 2 * 2 * H * NQ * N * D

F32 = mybir.dt.float32
BF16 = mybir.dt.bfloat16
U32 = mybir.dt.uint32
U8 = mybir.dt.uint8
FP8X4 = mybir.dt.float8_e4m3fn_x4
ACT = mybir.ActivationFunctionType
ALU = mybir.AluOpType

P = 128
PACK = 4
SIDE = 4
ROWS = P // SIDE
TILES = NQ // P
RUN = 4
EPS = 16.0 * 16.0 * 1e-5
SKEW = 3
SCALAR_PACKS = range(1, 6)


def tile_rows_a_silu_kb_onorm_kernel(tc, qT, kT, t, v, kb, gn, out):
    nc = tc.nc
    with ExitStack() as ctx:
        sb = ctx.enter_context(tc.tile_pool(name="sb", bufs=1))
        ps = ctx.enter_context(tc.psum_pool(name="ps", bufs=1))
        ctx.enter_context(tc.manual_schedule())

        def load_features(name, x, s, first, last):
            raw = sb.tile([P, PACK, last - first], F32, name=name)
            src = x[SIDE * s : SIDE * (s + 1)].rearrange("h (m j) n -> (h m) j n", j=PACK)
            nc.sync.dma_start(out=raw[:], in_=src[:, :, first:last])
            return raw

        def load_values(s):
            raw = sb.tile([P, SIDE, PACK * D], F32, name="v_raw%d" % s)
            src = v[SIDE * s : SIDE * (s + 1)].rearrange("h (m r) e -> m h (r e)", r=PACK)
            nc.sync.dma_start(out=raw[:], in_=src)
            return raw

        kb_sb = sb.tile([P, PACK], F32)
        t_sb = sb.tile([P, PACK], F32)
        gn_sb = sb.tile([P, D], F32)

        nc.scalar.dma_start(out=kb_sb[:], in_=kb.rearrange("(m r) o -> m (r o)", r=PACK))
        k_raw = [load_features("k_raw0", kT, 0, 0, N)]
        q0_halves = [load_features("q0_low", qT, 0, 0, NQ // 2)]
        nc.sync.dma_start(out=t_sb[:], in_=t.rearrange("(m r) o -> m (r o)", r=PACK))
        q0_halves.append(load_features("q0_high", qT, 0, NQ // 2, NQ))
        k_raw.append(load_features("k_raw1", kT, 1, 0, N))
        q1_raw = load_features("q1_raw", qT, 1, 0, NQ)
        v_raw = [load_values(0), load_values(1)]
        nc.sync.dma_start(out=gn_sb[:], in_=gn)

        packed, mx, p_sb, sums, roots = {}, {}, {}, {}, {}

        def deal_four(key, raw, a, copy):
            packed[key] = sb.tile([P, 2 * P * PACK], BF16, name="%s%d%d" % key, align_bytes=64)
            copy(
                out=packed[key][:].rearrange("p (r m j) -> p m j r", r=2, j=PACK),
                in_=raw[:].rearrange("p j (m r) -> p m j r", r=PACK)[:, :, :, 2 * a : 2 * a + 2],
            )

        def deal_two(key, raw):
            packed[key] = sb.tile([P, 2 * P * PACK], BF16, name="%s%d%d" % key, align_bytes=64)
            nc.vector.tensor_copy(
                out=packed[key][:].rearrange("p (c m n j) -> p m j n c", c=2, n=2, j=PACK),
                in_=raw[:].rearrange("p j (m n c) -> p m j n c", n=2, c=2),
            )

        def pack_values(h, copy):
            if h % 2 == 0:
                packed["v", 0, h] = sb.tile([P, 2 * D * PACK], BF16, name="v%d" % h, align_bytes=64)
            cols = slice(D * PACK * (h % 2), D * PACK * (h % 2 + 1))
            copy(
                out=packed["v", 0, h - h % 2][:, cols].rearrange("p (c i r) -> p c r i", i=RUN, r=PACK),
                in_=v_raw[h // SIDE][:, h % SIDE, :].rearrange("p (r c i) -> p c r i", r=PACK, i=RUN),
            )

        def quantize(key, skip, tiles):
            kind, group, first = key
            name = "%s%d%d" % (kind, group, first + skip)
            codes = sb.tile([P, tiles * P], U32, name=name + "_codes", align_bytes=64)
            scales = sb.tile([P, tiles * P], U8, name=name + "_scales", align_bytes=64)
            nc.vector.quantize_mx(
                out=codes[:].bitcast(FP8X4),
                scales=scales[:],
                in_=packed[key][:, P * PACK * skip : P * PACK * (skip + tiles)],
            )
            for x in range(tiles):
                cols = slice(P * x, P * (x + 1))
                mx[kind, group, first + skip + x] = (codes[:, cols], scales[:, cols])

        score_banks = []
        y_banks = []
        for g in range(SIDE):
            score_banks.append(ps.tile([P, PACK * P], F32, name="scores%d" % g))
            y_banks.append(ps.tile([P, TILES, D], F32, name="y%d" % g))

        def scores(h, places, first, tiles):
            s, g = divmod(h, SIDE)
            rows = slice(ROWS * g, ROWS * (g + 1))
            width = tiles * P
            for x, r in enumerate(places):
                k_codes, k_scales = mx["k", s, r]
                for c in range(tiles):
                    q_codes, q_scales = mx["q", s, first + c]
                    nc.tensor.matmul_mx(
                        out=score_banks[g][:, width * x + P * c : width * x + P * (c + 1)],
                        lhsT=k_codes[rows, :].bitcast(FP8X4),
                        lhsT_scale=k_scales[rows, :],
                        rhs=q_codes[rows, :].bitcast(FP8X4),
                        rhs_scale=q_scales[rows, :],
                        start=True,
                        stop=True,
                    )
            if places[0] == 0:
                p_sb[h, first] = sb.tile([P, PACK, width], F32, name="p%d%d" % (h, first))
            for x, r in enumerate(places):
                nc.scalar.activation(
                    out=p_sb[h, first][:, r, :],
                    in_=score_banks[g][:, width * x : width * (x + 1)],
                    func=ACT.Silu,
                    bias=kb_sb[:, r : r + 1],
                )

        def weigh(h, p_first, first, tiles):
            w = sb.tile([P, tiles * P * PACK], BF16, name="w", tag="w", bufs=3, align_bytes=64)
            packed["w", h, first] = w
            cols = slice(P * (first - p_first), P * (first - p_first + tiles))
            nc.vector.tensor_tensor(
                out=w[:].rearrange("p (c i r) -> p c r i", i=RUN, r=PACK),
                in0=p_sb[h, p_first][:, :, cols].rearrange("p r (c i) -> p c r i", i=RUN),
                in1=t_sb[:].unsqueeze(1).unsqueeze(3).to_broadcast([P, tiles * P // RUN, PACK, RUN]),
                op=ALU.mult,
            )

        def values(h):
            v_codes, v_scales = mx["v", 0, h]
            for j in range(TILES):
                w_codes, w_scales = mx["w", h, j]
                nc.tensor.matmul_mx(
                    out=y_banks[h % SIDE][:, j, :],
                    lhsT=w_codes.bitcast(FP8X4),
                    lhsT_scale=w_scales,
                    rhs=v_codes.bitcast(FP8X4),
                    rhs_scale=v_scales,
                    start=True,
                    stop=True,
                )

        def squares(h, first, last):
            if first == 0:
                sums[h] = sb.tile([P, TILES], F32, name="sums%d" % h)
            for j in range(first, last):
                square = sb.tile([P, D], F32, name="square", tag="square", bufs=4)
                nc.scalar.activation(
                    out=square[:],
                    in_=y_banks[h % SIDE][:, j, :],
                    func=ACT.Square,
                    accum_out=sums[h][:, j : j + 1],
                )

        def root(h, first, last):
            roots[h, first] = sb.tile([P, last - first], F32, name="roots%d%d" % (h, first))
            nc.scalar.activation(
                out=roots[h, first][:],
                in_=sums[h][:, first:last],
                func=ACT.Abs_reciprocal_sqrt,
                scale=1.0 / D,
                bias=EPS,
            )

        def finish(h, first, last):
            o = sb.tile([P, last - first, D], F32, name="o%d%d" % (h, first))
            for j in range(first, last):
                nc.vector.scalar_tensor_tensor(
                    out=o[:, j - first, :],
                    in0=y_banks[h % SIDE][:, j, :],
                    scalar=roots[h, first][:, j - first : j - first + 1],
                    in1=gn_sb[:],
                    op0=ALU.mult,
                    op1=ALU.mult,
                )
            if h < SIDE:
                nc.sync.dma_start(
                    out=out[h].rearrange("(u m c) e -> m u (c e)", u=2, c=2),
                    in_=o[:].rearrange("p (u c) e -> p u (c e)", c=2),
                )
            else:
                nc.sync.dma_start(out=out[h].rearrange("(m c) e -> m c e", c=TILES)[:, first:last, :], in_=o[:])

        front = []
        back = []

        def add_scores(h, places, first, tiles):
            s = h // SIDE
            needs = [("k", s, r) for r in places] + [("q", s, first + c) for c in range(tiles)]
            front.append((needs, [("p", h, first, places[-1])], scores, (h, places, first, tiles)))

        def add_values(h):
            needs = [("w", h, j) for j in range(TILES)] + [("v", 0, h)]
            if h >= SIDE:
                needs.append(("out", h - SIDE, 0))
            front.append((needs, [], values, (h,)))

        def add_squares(h, first, last):
            front.append(([], [], squares, (h, first, last)))

        def add_root(h, first, last):
            front.append(([], [("root", h, first)], root, (h, first, last)))

        def add_pack(program, h, copy):
            needs = [("packed v", h - 1)] if h % 2 else []
            program.append((needs, [("packed v", h)], pack_values, (h, copy)))

        def add_deal(key, raw, a):
            back.append(([], [], deal_four, (key, raw, a, nc.vector.tensor_copy)))

        def add_quantize(key, skip, tiles, needs):
            makes = [(key[0], key[1], key[2] + skip + x) for x in range(tiles)]
            back.append((needs, makes, quantize, (key, skip, tiles)))

        def add_quantize_values(h):
            add_quantize(("v", 0, h), 0, 2, [("packed v", h), ("packed v", h + 1)])

        def add_quantize_three(h):
            add_quantize(("w", h, 1), 0, 1, [])
            add_quantize(("w", h, 1), 1, 2, [])

        def add_weigh(h, p_first, first, tiles):
            back.append(([("p", h, p_first, PACK - 1)], [], weigh, (h, p_first, first, tiles)))

        def add_finish(h, first, last):
            back.append(([("root", h, first)], [("out", h, first)], finish, (h, first, last)))

        front.append(([], [("packed k",)], deal_four, (("k", 0, 2), k_raw[0], 1, nc.scalar.copy)))
        grid = {SIDE * h + SKEW * r: (h, r) for h in range(H) for r in range(PACK)}
        last_step = max(grid)
        for h in range(SIDE - 1):
            add_scores(h, list(range(PACK)), 0, 1)
        next_pack = SCALAR_PACKS.start
        for step in range(last_step + 1):
            if step in grid:
                h, r = grid[step]
                if step == last_step:
                    add_values(0)
                    add_squares(0, 0, TILES)
                first = 1 if h < SIDE else 0
                add_scores(h, [r], first, TILES - first)
                head_done = r == PACK - 1 and 3 <= h <= 5
                gap_opens = h == H - 1 and step + 1 not in grid and step < last_step
                if head_done or gap_opens:
                    add_pack(front, next_pack, nc.scalar.copy)
                    next_pack = next_pack + 1
            elif step == 1:
                add_scores(SIDE - 1, list(range(PACK)), 0, 1)
        assert next_pack == SCALAR_PACKS.stop
        for h in range(1, SIDE):
            add_values(h)
        add_root(0, 0, TILES)
        add_squares(1, 0, TILES)
        for h in range(1, H - 1):
            if h + 1 >= SIDE:
                add_values(h + 1)
            add_squares(h + 1, 0, 1)
            add_root(h, 0, TILES)
            add_squares(h + 1, 1, TILES if h + 1 < H - 1 else TILES - 1)
        add_root(H - 1, 0, TILES // 2)
        add_squares(H - 1, TILES - 1, TILES)
        add_root(H - 1, TILES // 2, TILES)

        add_deal(("k", 0, 0), k_raw[0], 0)
        add_quantize(("k", 0, 0), 0, 2, [])
        back.append(([], [], deal_two, (("q", 0, 0), q0_halves[0])))
        add_quantize(("k", 0, 2), 0, 2, [("packed k",)])
        add_quantize(("q", 0, 0), 0, 1, [])
        add_quantize(("q", 0, 0), 1, 1, [])
        back.append(([], [], deal_two, (("q", 0, 2), q0_halves[1])))
        add_quantize(("q", 0, 2), 0, 2, [])
        add_weigh(0, 0, 0, 1)
        add_deal(("k", 1, 0), k_raw[1], 0)
        add_quantize(("w", 0, 0), 0, 1, [])
        add_weigh(1, 0, 0, 1)
        add_deal(("k", 1, 2), k_raw[1], 1)
        add_quantize(("w", 1, 0), 0, 1, [])
        add_weigh(2, 0, 0, 1)
        add_quantize(("k", 1, 0), 0, 2, [])
        add_weigh(3, 0, 0, 1)
        add_quantize(("w", 2, 0), 0, 1, [])
        add_quantize(("k", 1, 2), 0, 2, [])
        add_deal(("q", 1, 0), q1_raw, 0)
        add_quantize(("w", 3, 0), 0, 1, [])
        add_deal(("q", 1, 2), q1_raw, 1)
        add_quantize(("q", 1, 0), 0, 2, [])
        add_quantize(("q", 1, 2), 0, 2, [])
        for h in range(SCALAR_PACKS.start):
            add_pack(back, h, nc.vector.tensor_copy)
        add_weigh(0, 1, 1, TILES - 1)
        for h in range(1, SIDE):
            add_weigh(h, 1, 1, TILES - 1)
            add_quantize_three(h - 1)
        for h in range(SCALAR_PACKS.stop, H):
            add_pack(back, h, nc.vector.tensor_copy)
        add_quantize_three(SIDE - 1)
        add_quantize_values(0)
        add_quantize_values(6)
        add_weigh(4, 0, 0, TILES)
        for h in range(5, H - 1):
            add_weigh(h, 0, 0, TILES)
            add_quantize(("w", h - 1, 0), 0, TILES, [])
            add_quantize_values(2 * (h - SIDE))
        add_weigh(H - 1, 0, 0, 2)
        add_quantize(("w", H - 2, 0), 0, TILES, [])
        add_finish(0, 0, TILES)
        add_finish(1, 0, TILES)
        add_quantize(("w", H - 1, 0), 0, 2, [])
        add_finish(2, 0, TILES)
        add_weigh(H - 1, 0, 2, 2)
        add_finish(3, 0, TILES)
        add_quantize(("w", H - 1, 2), 0, 2, [])
        for h in range(SIDE, H - 1):
            add_finish(h, 0, TILES)
        add_finish(H - 1, 0, TILES // 2)
        add_finish(H - 1, TILES // 2, TILES)

        made = set()
        programs = [front, back]
        done = [0, 0]
        while done[0] < len(front) or done[1] < len(back):
            for x, program in enumerate(programs):
                while done[x] < len(program) and all(need in made for need in program[done[x]][0]):
                    entry = program[done[x]]
                    entry[2](*entry[3])
                    for key in entry[1]:
                        made.add(key)
                    done[x] = done[x] + 1
